import numpy as np
import ml_dtypes


def mxq(x, axis, fmt="e4m3"):
    dtype, down = {"e4m3": (ml_dtypes.float8_e4m3fn, 7), "e5m2": (ml_dtypes.float8_e5m2, 14)}[fmt]
    v = np.moveaxis(np.asarray(x, np.float32).astype(ml_dtypes.bfloat16).astype(np.float64), axis, -1)
    blocks = v.reshape(v.shape[:-1] + (-1, 32))
    amax = np.abs(blocks).max(-1, keepdims=True)
    byte = np.maximum(np.where(amax > 0, np.frexp(amax)[1] - 1 + 127, 0) - down, 1)
    scale = np.exp2(byte - 127.0)
    codes = (blocks / scale).astype(np.float32).astype(dtype).astype(np.float64)
    return np.moveaxis((codes * scale).reshape(v.shape), -1, axis)


WIDE = False


def mx_kscale(k):
    if not WIDE:
        return np.ones(k)
    levels = np.array([10, -10, 5, -5, 0])
    if k % 512:
        return np.exp2(np.random.permutation(np.resize(levels, k // 32))).repeat(32)
    a = np.empty((k // 512, 16))
    for p in range(k // 512):
        a[p, :8] = np.random.permutation(np.resize(levels, 8))
        for g in range(8):
            far = levels[np.abs(levels - a[p, g]) >= 10]
            a[p, g + 8] = far[np.random.randint(len(far))]
    return np.exp2(a.ravel()).repeat(32)


BF16 = ml_dtypes.bfloat16


def bf(x):
    return np.asarray(x, np.float32).astype(BF16)


def f64(x):
    return np.asarray(x).astype(np.float64)


E2M1 = np.array([0.0, 0.5, 1.0, 1.5, 2.0, 3.0, 4.0, 6.0, -0.0, -0.5, -1.0, -1.5, -2.0, -3.0, -4.0, -6.0])


def pack_weight(w, fmt):
    k, n = w.shape
    w = f64(bf(w)).reshape(k // 32, 32, n)
    amax = np.abs(w).max(1)
    if fmt == "e4m3":
        byte = np.frexp(amax)[1] - 1 + 127 - 7
    else:
        mant, ex = np.frexp(amax / 6.0)
        byte = np.where(mant > 0.5, ex, ex - 1) + 127
    byte = np.clip(np.where(amax > 0, byte, 1), 1, 254)
    scaled = (w * np.exp2(127.0 - byte)[:, None, :]).reshape(k, n).astype(np.float32)
    by_word = np.ascontiguousarray(scaled.reshape(k // 512, 128, 4, n).transpose(0, 1, 3, 2))
    if fmt == "e4m3":
        words = by_word.astype(ml_dtypes.float8_e4m3fn).view(np.uint8)
    else:
        c = by_word.astype(ml_dtypes.float4_e2m1fn).view(np.uint8) & 0xF
        words = c[..., 0::2] | (c[..., 1::2] << 4)
    return np.ascontiguousarray(words), np.ascontiguousarray(byte.astype(np.uint8).reshape(k // 512, 16, n))


def unpack_weight(words, scales, fmt):
    g, p, n, _ = words.shape
    if fmt == "e4m3":
        vals = np.ascontiguousarray(words).view(ml_dtypes.float8_e4m3fn).astype(np.float64)
    else:
        nib = np.empty((g, p, n, 4), np.uint8)
        nib[..., 0::2] = words & 0xF
        nib[..., 1::2] = words >> 4
        vals = E2M1[nib]
    vals = vals * np.repeat(np.exp2(scales.astype(np.float64) - 127.0), 8, axis=1)[..., None]
    return vals.transpose(0, 1, 3, 2).reshape(g * 512, n)

E4M3FN = np.array([(-1.0 if i & 128 else 1.0) * ((1.0 + (i & 7) / 8.0) * 2.0 ** (((i >> 3) & 15) - 7) if i & 120 else (i & 7) * 2.0 ** -9) for i in range(256)])


def e4m3fn_bytes(y):
    return np.clip(np.asarray(y, np.float64), -448.0, 448.0).astype(np.float32).astype(ml_dtypes.float8_e4m3fn).view(np.uint8)


def e4m3fn_values(b):
    return E4M3FN[b]


N, D, K = 1024, 1024, 512


def stable_softplus(z):
    return np.maximum(z, 0.0) + np.log(1.0 + np.exp(-np.abs(z)))


def draw0():
    s, t = mx_kscale(D), mx_kscale(D)
    root_d = np.sqrt(D)
    x = bf(np.random.standard_normal((N, D)) * s)
    dt = bf(np.random.uniform(0.3, 2.0, (N,)))
    wc_words, wc_scales = pack_weight(np.random.standard_normal((D, D)) * 1.5 / root_d / s[:, None], "e4m3")
    wb_words, wb_scales = pack_weight(np.random.standard_normal((D, D)) * 1.5 / root_d / s[:, None], "e4m3")
    wd_words, wd_scales = pack_weight(np.random.standard_normal((D, D)) * 1.0 / root_d / s[:, None], "e4m3")
    g = bf((1.0 + 0.1 * np.random.standard_normal(D)) * t)
    wl_words, wl_scales = pack_weight(np.random.standard_normal((D, K)) * 2.0 / root_d / t[:, None], "e4m3")
    return {
        "x": x,
        "dt": dt,
        "wc_words": wc_words,
        "wc_scales": wc_scales,
        "wb_words": wb_words,
        "wb_scales": wb_scales,
        "wd_words": wd_words,
        "wd_scales": wd_scales,
        "g": g,
        "wl_words": wl_words,
        "wl_scales": wl_scales,
    }


def core(x, dt, wc_words, wc_scales, wb_words, wb_scales, wd_words, wd_scales, g, wl_words, wl_scales):
    xq = mxq(f64(x), 1, "e4m3")
    c0 = xq @ unpack_weight(wc_words, wc_scales, "e4m3")
    cbar = xq @ unpack_weight(wb_words, wb_scales, "e4m3")
    rate = stable_softplus(xq @ unpack_weight(wd_words, wd_scales, "e4m3"))
    c = cbar + (c0 - cbar) * np.exp(-rate * f64(dt)[:, None])
    h = f64(g)[None, :] * np.tanh(c)
    z = mxq(h, 1, "e4m3") @ unpack_weight(wl_words, wl_scales, "e4m3")
    return stable_softplus(z)


def setup_inputs():
    drawn = draw0()
    full = np.asarray(drawn['x']).astype(np.float64)
    scale = (np.abs(full).reshape(1024, 8, 128).max(axis=(2,)) / 448.0).astype(np.float32)
    given = {}
    for key, value in drawn.items():
        if key == 'x':
            given['x_bytes'] = e4m3fn_bytes(full / np.repeat(scale.astype(np.float64), 128, axis=1))
            given['x_scale'] = scale
        else:
            given[key] = value
    return given


def reference(x_bytes, x_scale, dt, wc_words, wc_scales, wb_words, wb_scales, wd_words, wd_scales, g, wl_words, wl_scales):
    return core(e4m3fn_values(x_bytes) * np.repeat(x_scale.astype(np.float64), 128, axis=1), dt, wc_words, wc_scales, wb_words, wb_scales, wd_words, wd_scales, g, wl_words, wl_scales)

@@ -1,0 +1,284 @@
+from contextlib import ExitStack
+
+import concourse.mybir as mybir
+from concourse.masks import make_identity
+
+N, D, K = 1024, 1024, 512
+FLOPS = 2 * N * D * (3 * D + K)
+
+F32 = mybir.dt.float32
+BF16 = mybir.dt.bfloat16
+I32 = mybir.dt.int32
+U32 = mybir.dt.uint32
+U8 = mybir.dt.uint8
+FP8 = mybir.dt.float8_e4m3fn
+FP8X4 = mybir.dt.float8_e4m3fn_x4
+ACT = mybir.ActivationFunctionType
+ALU = mybir.AluOpType
+
+P = 128
+TILES = N // P
+HALF = 512
+TINY = 2.0 ** -62
+BANKS = {'turn': ('bank', 8), 'mm': ('bank', 8), 'marks': ('bank', 8)}
+XT_SCALAR = (2, 3, 4, 5, 6)
+HT_SCALAR = (0, 1, 2, 3, 6)
+GAIN_POOL = (0, 1, 3, 6, 7)
+SUM_VECTOR = (4, 5, 7)
+CA = 6
+PLAN = (('cell_mix', 19.0, 1), ('widen_x', -2.25, 1), ('rate_sigmoid', 0.25, 1), ('collect_x', -1.5, 1), ('cell_sum', 20.0, 1), ('rate_mm_again', 12.5, 0.5), ('mark_mm', 27.5, 1), ('rate_min', 14.25, 0.5), ('rate_mm', -0.5, 1), ('decay', 17.0, 1.25), ('quantize_h', 25.25, 1), ('squash', 22.75, 0.75), ('turn_x', -2.0, 1), ('turn_h', 25.0, 1), ('mark_sigmoid', 27.75, 1), ('collect_h', 25.0, 1), ('cell_mm', 18.75, 1), ('gain_mul', 24.25, 0.75), ('rate_ln', 8.5, 0.75), ('quantize_x', -1.0, 1))
+
+
+def tile_neuralhawkesdecayingcellintensity_d1p_kernel(
+    tc, x_bytes, x_scale, dt, wc_words, wc_scales, wb_words, wb_scales, wd_words, wd_scales, g, wl_words, wl_scales, out
+):
+    nc = tc.nc
+    with ExitStack() as ctx:
+        keep = ctx.enter_context(tc.tile_pool(name="keep", bufs=1))
+        work = ctx.enter_context(tc.tile_pool(name="work", bufs=3))
+        psum = ctx.enter_context(tc.psum_pool(name="psum", bufs=8))
+        ctx.enter_context(tc.manual_schedule())
+
+        planes = {}
+        for w, width in (("d", D), ("c", D), ("b", D), ("l", K)):
+            planes[w] = keep.tile([P, width], U8, name="planes_" + w, align_bytes=64)
+        nc.gpsimd.memset(planes["d"][:].bitcast(I32), 0)
+        ident = keep.tile([P, P], F32, name="ident")
+        make_identity(nc, ident[:])
+        for w in ("c", "b", "l"):
+            nc.gpsimd.memset(planes[w][:].bitcast(I32), 0)
+        tiny = keep.tile([P, 1], F32, name="tiny")
+        nc.vector.memset(tiny[:], TINY)
+        warm = keep.tile([P, 1], F32, name="warm")
+        nc.scalar.activation(out=warm[:], in_=tiny[:], func=ACT.Sigmoid)
+
+        x_rows = x_bytes.rearrange("(p i) k -> p i k", i=TILES)
+        out_rows = out.rearrange("(p i) n -> p i n", i=TILES)
+        x_at = {}
+
+        def load_x(i0, count):
+            t = keep.tile([P, count, D], U8, name="xb%d" % i0, align_bytes=64)
+            nc.sync.dma_start(out=t[:], in_=x_rows[:, i0 : i0 + count, :])
+            for c in range(count):
+                x_at[i0 + c] = (t, c)
+
+        def load_scales(w, scales):
+            for q in range(4):
+                nc.sync.dma_start(
+                    out=planes[w][32 * q : 32 * q + 8, :].bitcast(I32),
+                    in_=scales[:, 4 * q : 4 * q + 4, :].bitcast(I32),
+                )
+
+        w_at = {}
+
+        def load_words(w, words, c_from, c_to, cols):
+            src = words.rearrange("g p n t -> p g (n t)").bitcast(I32)
+            for c0 in range(c_from, c_to, cols):
+                t = keep.tile([P, 2, cols], U32, name="w_%s%d" % (w, c0), align_bytes=64)
+                nc.sync.dma_start(out=t[:].bitcast(I32), in_=src[:, :, c0 : c0 + cols])
+                for h in range(cols // HALF):
+                    w_at[(w, c0 // HALF + h)] = (t, h)
+
+        load_x(0, 1)
+        xs = keep.tile([P, TILES, 8], F32, name="xs")
+        nc.sync.dma_start(out=xs[:], in_=x_scale.rearrange("(p i) j -> p i j", i=TILES))
+        load_scales("d", wd_scales)
+        load_words("d", wd_words, 0, HALF, HALF)
+        load_x(1, 3)
+        load_words("d", wd_words, HALF, D, HALF)
+        load_x(4, 4)
+        dt_bf = keep.tile([P, TILES], BF16, name="dt_bf")
+        nc.sync.dma_start(out=dt_bf[:], in_=dt.rearrange("(p i) -> p i", i=TILES))
+        load_scales("c", wc_scales)
+        load_words("c", wc_words, 0, D, D)
+        load_scales("b", wb_scales)
+        load_words("b", wb_words, 0, D, D)
+        load_scales("l", wl_scales)
+        load_words("l", wl_words, 0, K, K)
+        gain = keep.tile([P, D], BF16, name="gain")
+        nc.sync.dma_start(out=gain[:], in_=g.partition_broadcast(P))
+        dt_f = keep.tile([P, TILES], F32, name="dt_f")
+
+        e = [keep.tile([P, D], F32, name="e%d" % i) for i in range(TILES)]
+        e2 = keep.tile([P, TILES, K], F32, name="e2")
+        xq = [keep.tile([P, 256], U32, name="xq%d" % i, align_bytes=64) for i in range(TILES)]
+        xq_s = [keep.tile([P, 256], U8, name="xqs%d" % i, align_bytes=64) for i in range(TILES)]
+        hq = [keep.tile([P, 256], U32, name="hq%d" % i, align_bytes=64) for i in range(TILES)]
+        hq_s = [keep.tile([P, 256], U8, name="hqs%d" % i, align_bytes=64) for i in range(TILES)]
+        zs = {}
+        zr = {}
+        cc = {}
+        zm = {}
+        xw = {}
+        xt = {}
+        xg = {}
+        ht = {}
+        hg = {}
+        hh = {}
+        ca = {}
+        cb = {}
+
+        def bank(kind):
+            tag, bufs = BANKS[kind]
+            t = psum.tile([P, HALF], F32, name=tag, bufs=bufs)
+            return t
+
+        def widen(i, on_scalar):
+            t, c = x_at[i]
+            w = work.tile([P, D], BF16, name="xw", align_bytes=64)
+            xw[i] = w
+            for j in range(8):
+                cols = slice(128 * j, 128 * j + 128)
+                src = t[:, c, cols].bitcast(FP8)
+                if j in on_scalar:
+                    nc.scalar.activation(out=w[:, cols], in_=src, func=ACT.Copy, scale=xs[:, i, j : j + 1])
+                else:
+                    nc.vector.tensor_scalar(
+                        out=w[:, cols], in0=src, scalar1=xs[:, i, j : j + 1], scalar2=None, op0=ALU.mult
+                    )
+
+        def turn(rows):
+            t = bank("turn")
+            words = rows[:].bitcast(F32)
+            for gg in range(2):
+                for u in range(2):
+                    k = 2 * gg + u
+                    nc.tensor.transpose(
+                        t[:, 128 * k : 128 * k + 128], words[:, 256 * gg + u : 256 * gg + 256 : 2], ident[:]
+                    )
+            return t
+
+        def collect(t, name, copy):
+            o = work.tile([P, D], BF16, name=name, align_bytes=64)
+            copy(
+                out=o[:].bitcast(F32).rearrange("p (g r u) -> p g r u", g=2, u=2),
+                in_=t[:].rearrange("p (g u r) -> p g r u", g=2, u=2),
+            )
+            return o
+
+        def quantize(codes, scales, src):
+            nc.vector.quantize_mx(out=codes[:].bitcast(FP8X4), scales=scales[:], in_=src[:])
+
+        def multiply(codes, scales, w, h):
+            t = bank("marks" if w == "l" else "mm")
+            for gg in range(2):
+                wt, wh = w_at[(w, h)]
+                rows = slice(4 * gg, P)
+                nc.tensor.matmul_mx(
+                    out=t[:],
+                    lhsT=codes[:, 128 * gg : 128 * gg + 128].bitcast(FP8X4),
+                    lhsT_scale=scales[:, 128 * gg : 128 * gg + 128],
+                    rhs=wt[:, gg, HALF * wh : HALF * wh + HALF].bitcast(FP8X4),
+                    rhs_scale=planes[w][rows, HALF * h : HALF * h + HALF],
+                    start=(gg == 0),
+                    stop=(gg == 1),
+                )
+            return t
+
+        halves = (slice(0, HALF), slice(HALF, D))
+
+        def copier(i, on_scalar):
+            return nc.scalar.copy if i in on_scalar else nc.vector.tensor_copy
+
+        def widen_x(i):
+            widen(i, (4, 5, 6, 7) if i == 0 else ())
+
+        def turn_x(i):
+            xt[i] = turn(xw[i])
+
+        def collect_x(i):
+            xg[i] = collect(xt[i], "xg", copier(i, XT_SCALAR))
+
+        def quantize_x(i):
+            quantize(xq[i], xq_s[i], xg[i])
+
+        def rate_mm(i):
+            zs[i] = [multiply(xq[i], xq_s[i], "d", h) for h in range(2)]
+
+        def rate_sigmoid(i):
+            for h in range(2):
+                nc.scalar.activation(out=e[i][:, halves[h]], in_=zs[i][h][:], func=ACT.Sigmoid, scale=-1.0)
+
+        def rate_ln(i):
+            nc.scalar.activation(out=e[i][:], in_=e[i][:], func=ACT.Ln, bias=tiny[:])
+
+        def rate_mm_again(i):
+            zr[i] = [multiply(xq[i], xq_s[i], "d", h) for h in range(2)]
+
+        def rate_min(i):
+            if i == 0:
+                nc.vector.tensor_copy(out=dt_f[:], in_=dt_bf[:])
+            for h in range(2):
+                nc.vector.scalar_tensor_tensor(
+                    out=e[i][:, halves[h]], in0=zr[i][h][:], scalar=-1.0, in1=e[i][:, halves[h]], op0=ALU.mult, op1=ALU.min
+                )
+
+        def decay(i):
+            nc.scalar.activation(out=e[i][:], in_=e[i][:], func=ACT.Exp, scale=dt_f[:, i : i + 1])
+
+        def cell_mm(i):
+            cc[i] = [multiply(xq[i], xq_s[i], w, h) for h in range(2) for w in ("c", "b")]
+
+        def cell_mix(i):
+            a = work.tile([P, D], F32, name="ca", bufs=CA)
+            b = work.tile([P, D], F32, name="cb", bufs=3)
+            for h in range(2):
+                nc.vector.tensor_tensor(out=a[:, halves[h]], in0=cc[i][2 * h][:], in1=e[i][:, halves[h]], op=ALU.mult)
+                nc.vector.scalar_tensor_tensor(
+                    out=b[:, halves[h]], in0=e[i][:, halves[h]], scalar=1.0, in1=cc[i][2 * h + 1][:], op0=ALU.subtract, op1=ALU.mult
+                )
+            ca[i] = a
+            cb[i] = b
+
+        def cell_sum(i):
+            eng = nc.vector if i in SUM_VECTOR else nc.gpsimd
+            eng.tensor_tensor(out=ca[i][:], in0=ca[i][:], in1=cb[i][:], op=ALU.subtract)
+
+        def squash(i):
+            nc.scalar.activation(out=ca[i][:], in_=ca[i][:], func=ACT.Tanh)
+
+        def gain_mul(i):
+            hh[i] = work.tile([P, D], BF16, name="hh", align_bytes=64)
+            eng = nc.gpsimd if i in GAIN_POOL else nc.vector
+            eng.tensor_tensor(out=hh[i][:], in0=ca[i][:], in1=gain[:], op=ALU.mult)
+
+        def turn_h(i):
+            ht[i] = turn(hh[i])
+
+        def collect_h(i):
+            hg[i] = collect(ht[i], "hg", copier(i, HT_SCALAR))
+
+        def quantize_h(i):
+            quantize(hq[i], hq_s[i], hg[i])
+
+        def mark_mm(i):
+            zm[i] = multiply(hq[i], hq_s[i], "l", 0)
+
+        def mark_sigmoid(i):
+            nc.scalar.activation(out=e2[:, i, :], in_=zm[i][:], func=ACT.Sigmoid, scale=-1.0)
+
+        stages = dict(
+            widen_x=widen_x, turn_x=turn_x, collect_x=collect_x, quantize_x=quantize_x, rate_mm=rate_mm,
+            rate_sigmoid=rate_sigmoid, rate_ln=rate_ln, rate_mm_again=rate_mm_again, rate_min=rate_min, decay=decay,
+            cell_mm=cell_mm, cell_mix=cell_mix, cell_sum=cell_sum, squash=squash, gain_mul=gain_mul, turn_h=turn_h,
+            collect_h=collect_h, quantize_h=quantize_h, mark_mm=mark_mm, mark_sigmoid=mark_sigmoid,
+        )
+        events = sorted(
+            (first + stride * i, pos, name, i)
+            for pos, (name, first, stride) in enumerate(PLAN)
+            for i in range(TILES)
+        )
+        for step, pos, name, i in events:
+            stages[name](i)
+
+        for i0, count in ((0, 2), (2, 2), (4, 2), (6, 1), (7, 1)):
+            nc.scalar.activation(
+                out=e2[:, i0 : i0 + count, :], in_=e2[:, i0 : i0 + count, :], func=ACT.Ln, bias=tiny[:]
+            )
+            o = work.tile([P, 2, K], F32, name="o", bufs=5)
+            for c in range(count):
+                z2 = multiply(hq[i0 + c], hq_s[i0 + c], "l", 0)
+                nc.vector.scalar_tensor_tensor(
+                    out=o[:, c, :], in0=e2[:, i0 + c, :], scalar=-1.0, in1=z2[:], op0=ALU.mult, op1=ALU.max
+                )
+            nc.sync.dma_start(out=out_rows[:, i0 : i0 + count, :], in_=o[:, 0:count, :])

@@ -20,13 +20,22 @@ P = 128
 TILES = N // P
 HALF = 512
 TINY = 2.0 ** -62
-BANKS = {'turn': ('bank', 8), 'mm': ('bank', 8), 'marks': ('bank', 8)}
-XT_SCALAR = (2, 3, 4, 5, 6)
-HT_SCALAR = (0, 1, 2, 3, 6)
-GAIN_POOL = (0, 1, 3, 6, 7)
-SUM_VECTOR = (4, 5, 7)
+X_PERM = (1, 2, 3, 4, 5, 6, 7)
+H_PERM = (0, 1, 2, 3, 4, 5, 6, 7)
+Z_HELD = ()
+M_HELD = ()
+P2_ORDER = (5, 6, 7, 0, 1, 2, 3, 4)
+FIRST_MIN = 5
+TAIL = ((0, 2), (2, 2), (4, 2), (6, 1), (7, 1))
+BANKS = {'rate': ('mm', 5), 'again': ('mm', 5), 'cell': ('mm', 5), 'turn': ('turn', 3), 'marks': ('turn', 3)}
+XT_SCALAR = (1, 2, 3, 4)
+HT_SCALAR = (0, 1, 2, 5)
+GAIN_POOL = (2, 3)
+SUM_VECTOR = (4,)
+DIFF = (0, 1, 2, 3, 5, 6, 7)
 CA = 6
-PLAN = (('cell_mix', 19.0, 1), ('widen_x', -2.25, 1), ('rate_sigmoid', 0.25, 1), ('collect_x', -1.5, 1), ('cell_sum', 20.0, 1), ('rate_mm_again', 12.5, 0.5), ('mark_mm', 27.5, 1), ('rate_min', 14.25, 0.5), ('rate_mm', -0.5, 1), ('decay', 17.0, 1.25), ('quantize_h', 25.25, 1), ('squash', 22.75, 0.75), ('turn_x', -2.0, 1), ('turn_h', 25.0, 1), ('mark_sigmoid', 27.75, 1), ('collect_h', 25.0, 1), ('cell_mm', 18.75, 1), ('gain_mul', 24.25, 0.75), ('rate_ln', 8.5, 0.75), ('quantize_x', -1.0, 1))
+XG = 4
+PLAN = (('widen_x', (-19.3, -3.2), 0.5), ('turn_x', (-12.5, 4.1), 0.25), ('collect_x', (-4.2, 4.3), 0.75), ('quantize_x', (2.5, 4.6), 1), ('rate_mm', (3.15, 5.45), 1.25), ('rate_sigmoid', (5.25, 6.45), 1), ('negate_x', (3.5, 5.2), 1.25), ('quantize_neg', (14.2, 18.5), 0.75), ('rate_mm_again', (9.8, 12.6), 0.75), ('rate_ln', (10.0, 13.6), 0.5), ('rate_min', (12.0, 15.4), 0.75), ('decay', (16.9, 22.1), 0.25), ('cell_mm', (17.0, 23.2), 0.75), ('cell_mix', (18.9, 23.9), 1), ('cell_sum', (18.9, 25.2), 1), ('squash', (20.3, 25.4), 1.25), ('gain_mul', (22.9, 27.4), 1.25), ('turn_h', (25.2, 28.6), 1.25), ('collect_h', (27.0, 29.4), 1), ('quantize_h', (28.9, 34.7), 0.5), ('mark_mm', (30.5, 39.6), 0.25), ('mark_sigmoid', (36.5, 73.4), 0.75))
 
 
 def tile_neuralhawkesdecayingcellintensity_d1p_kernel(
@@ -37,7 +46,7 @@ def tile_neuralhawkesdecayingcellintensity_d1p_kernel(
         keep = ctx.enter_context(tc.tile_pool(name="keep", bufs=1))
         work = ctx.enter_context(tc.tile_pool(name="work", bufs=3))
         psum = ctx.enter_context(tc.psum_pool(name="psum", bufs=8))
-        ctx.enter_context(tc.manual_schedule())
+        ctx.enter_context(tc.manual_schedule(engines={mybir.EngineType.Activation, mybir.EngineType.SP, mybir.EngineType.PE}))
 
         planes = {}
         for w, width in (("d", D), ("c", D), ("b", D), ("l", K)):
@@ -97,6 +106,7 @@ def tile_neuralhawkesdecayingcellintensity_d1p_kernel(
         load_words("l", wl_words, 0, K, K)
         gain = keep.tile([P, D], BF16, name="gain")
         nc.sync.dma_start(out=gain[:], in_=g.partition_broadcast(P))
+        gain_perm = keep.tile([P, D], BF16, name="gain_perm")
         dt_f = keep.tile([P, TILES], F32, name="dt_f")
 
         e = [keep.tile([P, D], F32, name="e%d" % i) for i in range(TILES)]
@@ -106,6 +116,9 @@ def tile_neuralhawkesdecayingcellintensity_d1p_kernel(
         hq = [keep.tile([P, 256], U32, name="hq%d" % i, align_bytes=64) for i in range(TILES)]
         hq_s = [keep.tile([P, 256], U8, name="hqs%d" % i, align_bytes=64) for i in range(TILES)]
         zs = {}
+        xneg = {}
+        nq = {i: keep.tile([P, 256], U32, name="nq%d" % i, align_bytes=64) for i in DIFF}
+        nq_s = {i: keep.tile([P, 256], U8, name="nqs%d" % i, align_bytes=64) for i in DIFF}
         zr = {}
         cc = {}
         zm = {}
@@ -130,26 +143,33 @@ def tile_neuralhawkesdecayingcellintensity_d1p_kernel(
             for j in range(8):
                 cols = slice(128 * j, 128 * j + 128)
                 src = t[:, c, cols].bitcast(FP8)
+                o = w[:, cols]
+                if i in X_PERM:
+                    gg, m0 = j // 4, 32 * (j % 4)
+                    o = w[:].rearrange("p (g u m e) -> p g m u e", g=2, u=2, e=2)[:, gg, m0 : m0 + 32, :, :]
+                    src = src.rearrange("p (m u e) -> p m u e", u=2, e=2)
                 if j in on_scalar:
-                    nc.scalar.activation(out=w[:, cols], in_=src, func=ACT.Copy, scale=xs[:, i, j : j + 1])
+                    nc.scalar.activation(out=o, in_=src, func=ACT.Copy, scale=xs[:, i, j : j + 1])
                 else:
                     nc.vector.tensor_scalar(
-                        out=w[:, cols], in0=src, scalar1=xs[:, i, j : j + 1], scalar2=None, op0=ALU.mult
+                        out=o, in0=src, scalar1=xs[:, i, j : j + 1], scalar2=None, op0=ALU.mult
                     )
 
-        def turn(rows):
+        def turn(rows, perm):
             t = bank("turn")
             words = rows[:].bitcast(F32)
             for gg in range(2):
                 for u in range(2):
                     k = 2 * gg + u
-                    nc.tensor.transpose(
-                        t[:, 128 * k : 128 * k + 128], words[:, 256 * gg + u : 256 * gg + 256 : 2], ident[:]
-                    )
+                    if perm:
+                        picked = words[:, 128 * k : 128 * k + 128]
+                    else:
+                        picked = words[:, 256 * gg + u : 256 * gg + 256 : 2]
+                    nc.tensor.transpose(t[:, 128 * k : 128 * k + 128], picked, ident[:])
             return t
 
         def collect(t, name, copy):
-            o = work.tile([P, D], BF16, name=name, align_bytes=64)
+            o = work.tile([P, D], BF16, name=name, bufs=XG if name == "xg" else 3, align_bytes=64)
             copy(
                 out=o[:].bitcast(F32).rearrange("p (g r u) -> p g r u", g=2, u=2),
                 in_=t[:].rearrange("p (g u r) -> p g r u", g=2, u=2),
@@ -159,19 +179,21 @@ def tile_neuralhawkesdecayingcellintensity_d1p_kernel(
         def quantize(codes, scales, src):
             nc.vector.quantize_mx(out=codes[:].bitcast(FP8X4), scales=scales[:], in_=src[:])
 
-        def multiply(codes, scales, w, h):
-            t = bank("marks" if w == "l" else "mm")
-            for gg in range(2):
+        def multiply(operands, h, kind):
+            t = bank(kind)
+            last = 2 * len(operands) - 1
+            for k in range(last + 1):
+                (codes, scales), w = operands[k // 2]
+                gg = k % 2
                 wt, wh = w_at[(w, h)]
-                rows = slice(4 * gg, P)
                 nc.tensor.matmul_mx(
                     out=t[:],
                     lhsT=codes[:, 128 * gg : 128 * gg + 128].bitcast(FP8X4),
                     lhsT_scale=scales[:, 128 * gg : 128 * gg + 128],
                     rhs=wt[:, gg, HALF * wh : HALF * wh + HALF].bitcast(FP8X4),
-                    rhs_scale=planes[w][rows, HALF * h : HALF * h + HALF],
-                    start=(gg == 0),
-                    stop=(gg == 1),
+                    rhs_scale=planes[w][4 * gg : P, HALF * h : HALF * h + HALF],
+                    start=(k == 0),
+                    stop=(k == last),
                 )
             return t
 
@@ -184,7 +206,7 @@ def tile_neuralhawkesdecayingcellintensity_d1p_kernel(
             widen(i, (4, 5, 6, 7) if i == 0 else ())
 
         def turn_x(i):
-            xt[i] = turn(xw[i])
+            xt[i] = turn(xw[i], i in X_PERM)
 
         def collect_x(i):
             xg[i] = collect(xt[i], "xg", copier(i, XT_SCALAR))
@@ -192,8 +214,18 @@ def tile_neuralhawkesdecayingcellintensity_d1p_kernel(
         def quantize_x(i):
             quantize(xq[i], xq_s[i], xg[i])
 
+        def negate_x(i):
+            if i in DIFF:
+                n = work.tile([P, D], BF16, name="xn", align_bytes=64)
+                nc.vector.tensor_scalar(out=n[:], in0=xg[i][:], scalar1=-1.0, scalar2=None, op0=ALU.mult)
+                xneg[i] = n
+
+        def quantize_neg(i):
+            if i in DIFF:
+                quantize(nq[i], nq_s[i], xneg[i])
+
         def rate_mm(i):
-            zs[i] = [multiply(xq[i], xq_s[i], "d", h) for h in range(2)]
+            zs[i] = [multiply([((xq[i], xq_s[i]), "d")], h, "rate") for h in range(2)]
 
         def rate_sigmoid(i):
             for h in range(2):
@@ -203,11 +235,20 @@ def tile_neuralhawkesdecayingcellintensity_d1p_kernel(
             nc.scalar.activation(out=e[i][:], in_=e[i][:], func=ACT.Ln, bias=tiny[:])
 
         def rate_mm_again(i):
-            zr[i] = [multiply(xq[i], xq_s[i], "d", h) for h in range(2)]
+            if i in Z_HELD:
+                zr[i] = zs[i]
+                return
+            zr[i] = [multiply([((xq[i], xq_s[i]), "d")], h, "again") for h in range(2)]
 
         def rate_min(i):
-            if i == 0:
+            if i == FIRST_MIN:
                 nc.vector.tensor_copy(out=dt_f[:], in_=dt_bf[:])
+                if H_PERM:
+                    for gg in range(2):
+                        nc.vector.tensor_copy(
+                            out=gain_perm[:, halves[gg]].rearrange("p (u m e) -> p u m e", u=2, e=2),
+                            in_=gain[:, halves[gg]].rearrange("p (m u e) -> p u m e", u=2, e=2),
+                        )
             for h in range(2):
                 nc.vector.scalar_tensor_tensor(
                     out=e[i][:, halves[h]], in0=zr[i][h][:], scalar=-1.0, in1=e[i][:, halves[h]], op0=ALU.mult, op1=ALU.min
@@ -217,20 +258,34 @@ def tile_neuralhawkesdecayingcellintensity_d1p_kernel(
             nc.scalar.activation(out=e[i][:], in_=e[i][:], func=ACT.Exp, scale=dt_f[:, i : i + 1])
 
         def cell_mm(i):
-            cc[i] = [multiply(xq[i], xq_s[i], w, h) for h in range(2) for w in ("c", "b")]
+            cc[i] = []
+            x_plus = (xq[i], xq_s[i])
+            for h in range(2):
+                first = [(x_plus, "c")]
+                if i in DIFF:
+                    first.append(((nq[i], nq_s[i]), "b"))
+                cc[i].append(multiply(first, h, "cell"))
+                cc[i].append(multiply([(x_plus, "b")], h, "cell"))
 
         def cell_mix(i):
             a = work.tile([P, D], F32, name="ca", bufs=CA)
-            b = work.tile([P, D], F32, name="cb", bufs=3)
+            ca[i] = a
+            if i in DIFF:
+                for h in range(2):
+                    nc.vector.tensor_tensor(out=a[:, halves[h]], in0=cc[i][2 * h][:], in1=e[i][:, halves[h]], op=ALU.mult)
+                    nc.vector.tensor_tensor(out=a[:, halves[h]], in0=cc[i][2 * h + 1][:], in1=a[:, halves[h]], op=ALU.add)
+                return
+            b = work.tile([P, D], F32, name="cb", bufs=4)
             for h in range(2):
                 nc.vector.tensor_tensor(out=a[:, halves[h]], in0=cc[i][2 * h][:], in1=e[i][:, halves[h]], op=ALU.mult)
                 nc.vector.scalar_tensor_tensor(
                     out=b[:, halves[h]], in0=e[i][:, halves[h]], scalar=1.0, in1=cc[i][2 * h + 1][:], op0=ALU.subtract, op1=ALU.mult
                 )
-            ca[i] = a
             cb[i] = b
 
         def cell_sum(i):
+            if i in DIFF:
+                return
             eng = nc.vector if i in SUM_VECTOR else nc.gpsimd
             eng.tensor_tensor(out=ca[i][:], in0=ca[i][:], in1=cb[i][:], op=ALU.subtract)
 
@@ -238,12 +293,21 @@ def tile_neuralhawkesdecayingcellintensity_d1p_kernel(
             nc.scalar.activation(out=ca[i][:], in_=ca[i][:], func=ACT.Tanh)
 
         def gain_mul(i):
-            hh[i] = work.tile([P, D], BF16, name="hh", align_bytes=64)
+            hh[i] = work.tile([P, D], BF16, name="hh", bufs=4, align_bytes=64)
             eng = nc.gpsimd if i in GAIN_POOL else nc.vector
-            eng.tensor_tensor(out=hh[i][:], in0=ca[i][:], in1=gain[:], op=ALU.mult)
+            if i not in H_PERM:
+                eng.tensor_tensor(out=hh[i][:], in0=ca[i][:], in1=gain[:], op=ALU.mult)
+                return
+            for gg in range(2):
+                eng.tensor_tensor(
+                    out=hh[i][:, halves[gg]].rearrange("p (u m e) -> p u m e", u=2, e=2),
+                    in0=ca[i][:, halves[gg]].rearrange("p (m u e) -> p u m e", u=2, e=2),
+                    in1=gain_perm[:, halves[gg]].rearrange("p (u m e) -> p u m e", u=2, e=2),
+                    op=ALU.mult,
+                )
 
         def turn_h(i):
-            ht[i] = turn(hh[i])
+            ht[i] = turn(hh[i], i in H_PERM)
 
         def collect_h(i):
             hg[i] = collect(ht[i], "hg", copier(i, HT_SCALAR))
@@ -252,32 +316,34 @@ def tile_neuralhawkesdecayingcellintensity_d1p_kernel(
             quantize(hq[i], hq_s[i], hg[i])
 
         def mark_mm(i):
-            zm[i] = multiply(hq[i], hq_s[i], "l", 0)
+            zm[i] = multiply([((hq[i], hq_s[i]), "l")], 0, "cell" if i in M_HELD else "marks")
 
         def mark_sigmoid(i):
             nc.scalar.activation(out=e2[:, i, :], in_=zm[i][:], func=ACT.Sigmoid, scale=-1.0)
 
         stages = dict(
-            widen_x=widen_x, turn_x=turn_x, collect_x=collect_x, quantize_x=quantize_x, rate_mm=rate_mm,
+            widen_x=widen_x, turn_x=turn_x, collect_x=collect_x, quantize_x=quantize_x, negate_x=negate_x, quantize_neg=quantize_neg, rate_mm=rate_mm,
             rate_sigmoid=rate_sigmoid, rate_ln=rate_ln, rate_mm_again=rate_mm_again, rate_min=rate_min, decay=decay,
             cell_mm=cell_mm, cell_mix=cell_mix, cell_sum=cell_sum, squash=squash, gain_mul=gain_mul, turn_h=turn_h,
             collect_h=collect_h, quantize_h=quantize_h, mark_mm=mark_mm, mark_sigmoid=mark_sigmoid,
         )
         events = sorted(
-            (first + stride * i, pos, name, i)
+            (first[n // 4] + stride * (n % 4), pos, name, i)
             for pos, (name, first, stride) in enumerate(PLAN)
-            for i in range(TILES)
+            for n, i in enumerate(P2_ORDER if name in ("rate_ln", "rate_mm_again", "rate_min") else range(TILES))
         )
         for step, pos, name, i in events:
             stages[name](i)
 
-        for i0, count in ((0, 2), (2, 2), (4, 2), (6, 1), (7, 1)):
+        for i0, count in TAIL:
             nc.scalar.activation(
                 out=e2[:, i0 : i0 + count, :], in_=e2[:, i0 : i0 + count, :], func=ACT.Ln, bias=tiny[:]
             )
             o = work.tile([P, 2, K], F32, name="o", bufs=5)
             for c in range(count):
-                z2 = multiply(hq[i0 + c], hq_s[i0 + c], "l", 0)
+                z2 = zm[i0 + c]
+                if i0 + c not in M_HELD:
+                    z2 = multiply([((hq[i0 + c], hq_s[i0 + c]), "l")], 0, "again" if c else "cell")
                 nc.vector.scalar_tensor_tensor(
                     out=o[:, c, :], in0=e2[:, i0 + c, :], scalar=-1.0, in1=z2[:], op0=ALU.mult, op1=ALU.max
                 )

@@ -20,22 +20,28 @@ P = 128
 TILES = N // P
 HALF = 512
 TINY = 2.0 ** -62
-X_PERM = (1, 2, 3, 4, 5, 6, 7)
-H_PERM = (0, 1, 2, 3, 4, 5, 6, 7)
-Z_HELD = ()
-M_HELD = ()
-P2_ORDER = (5, 6, 7, 0, 1, 2, 3, 4)
-FIRST_MIN = 5
-TAIL = ((0, 2), (2, 2), (4, 2), (6, 1), (7, 1))
-BANKS = {'rate': ('mm', 5), 'again': ('mm', 5), 'cell': ('mm', 5), 'turn': ('turn', 3), 'marks': ('turn', 3)}
-XT_SCALAR = (1, 2, 3, 4)
-HT_SCALAR = (0, 1, 2, 5)
-GAIN_POOL = (2, 3)
-SUM_VECTOR = (4,)
-DIFF = (0, 1, 2, 3, 5, 6, 7)
-CA = 6
-XG = 4
-PLAN = (('widen_x', (-19.3, -3.2), 0.5), ('turn_x', (-12.5, 4.1), 0.25), ('collect_x', (-4.2, 4.3), 0.75), ('quantize_x', (2.5, 4.6), 1), ('rate_mm', (3.15, 5.45), 1.25), ('rate_sigmoid', (5.25, 6.45), 1), ('negate_x', (3.5, 5.2), 1.25), ('quantize_neg', (14.2, 18.5), 0.75), ('rate_mm_again', (9.8, 12.6), 0.75), ('rate_ln', (10.0, 13.6), 0.5), ('rate_min', (12.0, 15.4), 0.75), ('decay', (16.9, 22.1), 0.25), ('cell_mm', (17.0, 23.2), 0.75), ('cell_mix', (18.9, 23.9), 1), ('cell_sum', (18.9, 25.2), 1), ('squash', (20.3, 25.4), 1.25), ('gain_mul', (22.9, 27.4), 1.25), ('turn_h', (25.2, 28.6), 1.25), ('collect_h', (27.0, 29.4), 1), ('quantize_h', (28.9, 34.7), 0.5), ('mark_mm', (30.5, 39.6), 0.25), ('mark_sigmoid', (36.5, 73.4), 0.75))
+XT_S = (0, 1, 2)
+HT_S = (0, 1, 2, 3, 4, 5, 6, 7)
+DIFF = (1, 3, 5, 6, 7)
+GS = (0, 2, 4)
+GG = ()
+BUFS = {'xw': 4, 'xg': 5, 'xn': 2, 'ca': 5, 'cb': 4, 'hh': 4, 'hg': 2, 'o': 8}
+ORDER = """
+w.0 w.1 w.2 ws.0 t.0 t.1 k.0 q.0 t.2 k.1 q.1 w.3 k.2 q.2 w.4 w.5 z.0.0 s.0.0 z.0.1 s.0.1 t.3 k.3 q.3 x.0 w.6
+z.1.0 s.1.0 z.1.1 s.1.1 t.4 k.4 q.4 w.7 z.2.0 s.2.0 z.2.1 s.2.1 t.5 k.5 q.5 z.3.0 s.3.0 z.3.1 s.3.1 t.6 k.6
+q.6 n.1 z.4.0 s.4.0 z.4.1 s.4.1 t.7 k.7 q.7 nq.1 n.3 z.5.0 s.5.0 z.5.1 s.5.1 nq.3 z.6.0 s.6.0 z.6.1 s.6.1 n.5
+z.7.0 s.7.0 z.7.1 s.7.1 l.0 l.1 l.2 nq.5 l.3 n.6 l.4 l.5 nq.6 l.6 n.7 y.0.0 m.0.0 y.0.1 m.0.1 l.7 y.1.0 m.1.0
+y.1.1 m.1.1 e.0 nq.7 y.2.0 m.2.0 y.2.1 m.2.1 e.1 y.3.0 m.3.0 y.3.1 m.3.1 e.2 y.4.0 m.4.0 y.4.1 m.4.1 e.3 y.5.0
+m.5.0 y.5.1 m.5.1 e.4 y.6.0 m.6.0 y.6.1 m.6.1 e.5 y.7.0 m.7.0 y.7.1 m.7.1 X.0 e.6 c.0.0 a.0.0 c.0.1 a.0.1 e.7
+c.1.0 a.1.0 c.1.1 a.1.1 b.0.0 f.0.0 b.0.1 f.0.1 c.2.0 a.2.0 c.2.1 a.2.1 b.1.0 f.1.0 b.1.1 f.1.1 c.3.0 a.3.0
+c.3.1 a.3.1 b.2.0 f.2.0 b.2.1 f.2.1 b.3.0 f.3.0 b.3.1 f.3.1 c.4.0 a.4.0 c.4.1 a.4.1 b.4.0 f.4.0 b.4.1 f.4.1
+u.0 T.0 T.1 g.0.0 g.0.1 g.1.0 g.1.1 c.5.0 a.5.0 c.5.1 a.5.1 b.5.0 f.5.0 b.5.1 f.5.1 u.2 T.2 T.3 g.2.0 g.2.1
+h.0.0 h.0.1 j.0 p.0 c.6.0 a.6.0 c.6.1 a.6.1 g.3.0 g.3.1 h.1.0 h.1.1 b.6.0 f.6.0 b.6.1 f.6.1 u.4 T.4 j.1 p.1
+T.5 h.2.0 h.2.1 j.2 p.2 r.0 R.0 T.6 c.7.0 a.7.0 c.7.1 a.7.1 g.4.0 g.4.1 b.7.0 f.7.0 b.7.1 f.7.1 h.3.0 h.3.1
+j.3 p.3 r.1 R.1 T.7.0 T.7.1 g.5.0 g.5.1 g.6.0 g.6.1 h.4.0 h.4.1 j.4 p.4 r.2 R.2 g.7.0 g.7.1 h.5.0 h.5.1 j.5
+p.5 r.3 R.3 h.6.0 h.6.1 j.6 p.6 r.4 R.4 h.7.0 h.7.1 j.7 p.7 r.5 R.5 r.6 R.6 r.7 R.7 L.0 L.1 v.0 o.0 L.2 v.1
+o.1 L.3 v.2 o.2 L.4 v.3 o.3 L.5 v.4 o.4 L.6 v.5 o.5 o.6 L.7 o.7
+"""
 
 
 def tile_neuralhawkesdecayingcellintensity_d1p_kernel(
@@ -44,9 +50,9 @@ def tile_neuralhawkesdecayingcellintensity_d1p_kernel(
     nc = tc.nc
     with ExitStack() as ctx:
         keep = ctx.enter_context(tc.tile_pool(name="keep", bufs=1))
-        work = ctx.enter_context(tc.tile_pool(name="work", bufs=3))
+        work = ctx.enter_context(tc.tile_pool(name="work", bufs=4))
         psum = ctx.enter_context(tc.psum_pool(name="psum", bufs=8))
-        ctx.enter_context(tc.manual_schedule(engines={mybir.EngineType.Activation, mybir.EngineType.SP, mybir.EngineType.PE}))
+        ctx.enter_context(tc.manual_schedule())
 
         planes = {}
         for w, width in (("d", D), ("c", D), ("b", D), ("l", K)):
@@ -80,107 +86,120 @@ def tile_neuralhawkesdecayingcellintensity_d1p_kernel(
 
         w_at = {}
 
-        def load_words(w, words, c_from, c_to, cols):
+        def load_words(w, words, c_from, c_to):
             src = words.rearrange("g p n t -> p g (n t)").bitcast(I32)
-            for c0 in range(c_from, c_to, cols):
-                t = keep.tile([P, 2, cols], U32, name="w_%s%d" % (w, c0), align_bytes=64)
-                nc.sync.dma_start(out=t[:].bitcast(I32), in_=src[:, :, c0 : c0 + cols])
-                for h in range(cols // HALF):
-                    w_at[(w, c0 // HALF + h)] = (t, h)
+            t = keep.tile([P, 2, c_to - c_from], U32, name="w_%s%d" % (w, c_from), align_bytes=64)
+            nc.sync.dma_start(out=t[:].bitcast(I32), in_=src[:, :, c_from:c_to])
+            for h in range(c_from // HALF, c_to // HALF):
+                w_at[(w, h)] = (t, h - c_from // HALF)
 
-        load_x(0, 1)
+        load_x(0, 2)
         xs = keep.tile([P, TILES, 8], F32, name="xs")
         nc.sync.dma_start(out=xs[:], in_=x_scale.rearrange("(p i) j -> p i j", i=TILES))
         load_scales("d", wd_scales)
-        load_words("d", wd_words, 0, HALF, HALF)
-        load_x(1, 3)
-        load_words("d", wd_words, HALF, D, HALF)
+        load_words("d", wd_words, 0, HALF)
+        load_x(2, 2)
+        load_words("d", wd_words, HALF, D)
         load_x(4, 4)
         dt_bf = keep.tile([P, TILES], BF16, name="dt_bf")
         nc.sync.dma_start(out=dt_bf[:], in_=dt.rearrange("(p i) -> p i", i=TILES))
-        load_scales("c", wc_scales)
-        load_words("c", wc_words, 0, D, D)
-        load_scales("b", wb_scales)
-        load_words("b", wb_words, 0, D, D)
-        load_scales("l", wl_scales)
-        load_words("l", wl_words, 0, K, K)
         gain = keep.tile([P, D], BF16, name="gain")
+        gain_sorted = keep.tile([P, D], BF16, name="gain_sorted")
+        load_scales("c", wc_scales)
+        load_words("c", wc_words, 0, D)
+        load_scales("b", wb_scales)
+        load_words("b", wb_words, 0, D)
         nc.sync.dma_start(out=gain[:], in_=g.partition_broadcast(P))
-        gain_perm = keep.tile([P, D], BF16, name="gain_perm")
+        load_scales("l", wl_scales)
+        load_words("l", wl_words, 0, K)
         dt_f = keep.tile([P, TILES], F32, name="dt_f")
 
-        e = [keep.tile([P, D], F32, name="e%d" % i) for i in range(TILES)]
-        e2 = keep.tile([P, TILES, K], F32, name="e2")
-        xq = [keep.tile([P, 256], U32, name="xq%d" % i, align_bytes=64) for i in range(TILES)]
-        xq_s = [keep.tile([P, 256], U8, name="xqs%d" % i, align_bytes=64) for i in range(TILES)]
-        hq = [keep.tile([P, 256], U32, name="hq%d" % i, align_bytes=64) for i in range(TILES)]
-        hq_s = [keep.tile([P, 256], U8, name="hqs%d" % i, align_bytes=64) for i in range(TILES)]
-        zs = {}
-        xneg = {}
-        nq = {i: keep.tile([P, 256], U32, name="nq%d" % i, align_bytes=64) for i in DIFF}
-        nq_s = {i: keep.tile([P, 256], U8, name="nqs%d" % i, align_bytes=64) for i in DIFF}
-        zr = {}
-        cc = {}
-        zm = {}
-        xw = {}
-        xt = {}
-        xg = {}
-        ht = {}
-        hg = {}
-        hh = {}
-        ca = {}
-        cb = {}
+        def row(dtype, width, name):
+            return [keep.tile([P, width], dtype, name="%s%d" % (name, i), align_bytes=64) for i in range(TILES)]
 
-        def bank(kind):
-            tag, bufs = BANKS[kind]
-            t = psum.tile([P, HALF], F32, name=tag, bufs=bufs)
+        e = row(F32, D, "e")
+        e2 = row(F32, K, "e2")
+        xq = list(zip(row(U32, 256, "xq"), row(U8, 256, "xqs")))
+        nq = list(zip(row(U32, 256, "nq"), row(U8, 256, "nqs")))
+        hq = list(zip(row(U32, 256, "hq"), row(U8, 256, "hqs")))
+        at = {}
+        halves = (slice(0, HALF), slice(HALF, D))
+        ALL = slice(0, D)
+
+        def bank():
+            t = psum.tile([P, HALF], F32, name="bank")
             return t
 
-        def widen(i, on_scalar):
+        def widened(i):
+            if ("xw", i) not in at:
+                at["xw", i] = work.tile([P, D], BF16, name="xw", bufs=BUFS["xw"], align_bytes=64)
+            return at["xw", i]
+
+        def widen(i, blocks, on_scalar):
             t, c = x_at[i]
-            w = work.tile([P, D], BF16, name="xw", align_bytes=64)
-            xw[i] = w
-            for j in range(8):
+            w = widened(i)
+            for j in blocks:
                 cols = slice(128 * j, 128 * j + 128)
                 src = t[:, c, cols].bitcast(FP8)
                 o = w[:, cols]
-                if i in X_PERM:
+                if i > 0:
                     gg, m0 = j // 4, 32 * (j % 4)
                     o = w[:].rearrange("p (g u m e) -> p g m u e", g=2, u=2, e=2)[:, gg, m0 : m0 + 32, :, :]
                     src = src.rearrange("p (m u e) -> p m u e", u=2, e=2)
-                if j in on_scalar:
-                    nc.scalar.activation(out=o, in_=src, func=ACT.Copy, scale=xs[:, i, j : j + 1])
+                scale = xs[:, i, j : j + 1]
+                if on_scalar:
+                    nc.scalar.activation(out=o, in_=src, func=ACT.Copy, scale=scale)
                 else:
-                    nc.vector.tensor_scalar(
-                        out=o, in0=src, scalar1=xs[:, i, j : j + 1], scalar2=None, op0=ALU.mult
-                    )
+                    nc.vector.tensor_scalar(out=o, in0=src, scalar1=scale, scalar2=None, op0=ALU.mult)
 
-        def turn(rows, perm):
-            t = bank("turn")
+        def ev_w(i):
+            widen(i, range(8) if i else range(4), False)
+
+        def ev_ws(i):
+            widen(i, range(4, 8), True)
+
+        def turn(bank_tile, rows, gg, sorted_words):
             words = rows[:].bitcast(F32)
-            for gg in range(2):
-                for u in range(2):
-                    k = 2 * gg + u
-                    if perm:
-                        picked = words[:, 128 * k : 128 * k + 128]
-                    else:
-                        picked = words[:, 256 * gg + u : 256 * gg + 256 : 2]
-                    nc.tensor.transpose(t[:, 128 * k : 128 * k + 128], picked, ident[:])
-            return t
+            for u in range(2):
+                k = 2 * gg + u
+                if sorted_words:
+                    picked = words[:, 128 * k : 128 * k + 128]
+                else:
+                    picked = words[:, 256 * gg + u : 256 * gg + 256 : 2]
+                nc.tensor.transpose(bank_tile[:, 128 * k : 128 * k + 128], picked, ident[:])
 
-        def collect(t, name, copy):
-            o = work.tile([P, D], BF16, name=name, bufs=XG if name == "xg" else 3, align_bytes=64)
+        def ev_t(i):
+            at["xt", i] = bank()
+            for gg in range(2):
+                turn(at["xt", i], at["xw", i], gg, i > 0)
+
+        def collect(t, name, on_scalar):
+            o = work.tile([P, D], BF16, name=name, bufs=BUFS[name], align_bytes=64)
+            copy = nc.scalar.copy if on_scalar else nc.vector.tensor_copy
             copy(
                 out=o[:].bitcast(F32).rearrange("p (g r u) -> p g r u", g=2, u=2),
                 in_=t[:].rearrange("p (g u r) -> p g r u", g=2, u=2),
             )
             return o
 
-        def quantize(codes, scales, src):
-            nc.vector.quantize_mx(out=codes[:].bitcast(FP8X4), scales=scales[:], in_=src[:])
+        def quantize(q, src):
+            nc.vector.quantize_mx(out=q[0][:].bitcast(FP8X4), scales=q[1][:], in_=src[:])
 
-        def multiply(operands, h, kind):
-            t = bank(kind)
+        def ev_k(i):
+            at["xg", i] = collect(at["xt", i], "xg", i in XT_S)
+
+        def ev_q(i):
+            quantize(xq[i], at["xg", i])
+
+        def ev_n(i):
+            at["xn", i] = work.tile([P, D], BF16, name="xn", bufs=BUFS["xn"], align_bytes=64)
+            nc.vector.tensor_scalar(out=at["xn", i][:], in0=at["xg", i][:], scalar1=-1.0, scalar2=None, op0=ALU.mult)
+
+        def ev_nq(i):
+            quantize(nq[i], at["xn", i])
+
+        def multiply(operands, h):
+            t = bank()
             last = 2 * len(operands) - 1
             for k in range(last + 1):
                 (codes, scales), w = operands[k // 2]
@@ -197,154 +216,119 @@ def tile_neuralhawkesdecayingcellintensity_d1p_kernel(
                 )
             return t
 
-        halves = (slice(0, HALF), slice(HALF, D))
+        def ev_z(i, h):
+            at["z", i, h] = multiply([(xq[i], "d")], h)
 
-        def copier(i, on_scalar):
-            return nc.scalar.copy if i in on_scalar else nc.vector.tensor_copy
+        def ev_s(i, h):
+            nc.scalar.activation(out=e[i][:, halves[h]], in_=at["z", i, h][:], func=ACT.Sigmoid, scale=-1.0)
 
-        def widen_x(i):
-            widen(i, (4, 5, 6, 7) if i == 0 else ())
-
-        def turn_x(i):
-            xt[i] = turn(xw[i], i in X_PERM)
-
-        def collect_x(i):
-            xg[i] = collect(xt[i], "xg", copier(i, XT_SCALAR))
-
-        def quantize_x(i):
-            quantize(xq[i], xq_s[i], xg[i])
-
-        def negate_x(i):
-            if i in DIFF:
-                n = work.tile([P, D], BF16, name="xn", align_bytes=64)
-                nc.vector.tensor_scalar(out=n[:], in0=xg[i][:], scalar1=-1.0, scalar2=None, op0=ALU.mult)
-                xneg[i] = n
-
-        def quantize_neg(i):
-            if i in DIFF:
-                quantize(nq[i], nq_s[i], xneg[i])
-
-        def rate_mm(i):
-            zs[i] = [multiply([((xq[i], xq_s[i]), "d")], h, "rate") for h in range(2)]
-
-        def rate_sigmoid(i):
-            for h in range(2):
-                nc.scalar.activation(out=e[i][:, halves[h]], in_=zs[i][h][:], func=ACT.Sigmoid, scale=-1.0)
-
-        def rate_ln(i):
+        def ev_l(i):
             nc.scalar.activation(out=e[i][:], in_=e[i][:], func=ACT.Ln, bias=tiny[:])
 
-        def rate_mm_again(i):
-            if i in Z_HELD:
-                zr[i] = zs[i]
-                return
-            zr[i] = [multiply([((xq[i], xq_s[i]), "d")], h, "again") for h in range(2)]
+        def ev_y(i, h):
+            at["y", i, h] = multiply([(xq[i], "d")], h)
 
-        def rate_min(i):
-            if i == FIRST_MIN:
-                nc.vector.tensor_copy(out=dt_f[:], in_=dt_bf[:])
-                if H_PERM:
-                    for gg in range(2):
-                        nc.vector.tensor_copy(
-                            out=gain_perm[:, halves[gg]].rearrange("p (u m e) -> p u m e", u=2, e=2),
-                            in_=gain[:, halves[gg]].rearrange("p (m u e) -> p u m e", u=2, e=2),
-                        )
-            for h in range(2):
-                nc.vector.scalar_tensor_tensor(
-                    out=e[i][:, halves[h]], in0=zr[i][h][:], scalar=-1.0, in1=e[i][:, halves[h]], op0=ALU.mult, op1=ALU.min
-                )
+        def ev_m(i, h):
+            z = at["y", i, h] if ("y", i, h) in at else at["z", i, h]
+            nc.vector.scalar_tensor_tensor(
+                out=e[i][:, halves[h]], in0=z[:], scalar=-1.0, in1=e[i][:, halves[h]], op0=ALU.mult, op1=ALU.min
+            )
 
-        def decay(i):
+        def ev_e(i):
             nc.scalar.activation(out=e[i][:], in_=e[i][:], func=ACT.Exp, scale=dt_f[:, i : i + 1])
 
-        def cell_mm(i):
-            cc[i] = []
-            x_plus = (xq[i], xq_s[i])
-            for h in range(2):
-                first = [(x_plus, "c")]
-                if i in DIFF:
-                    first.append(((nq[i], nq_s[i]), "b"))
-                cc[i].append(multiply(first, h, "cell"))
-                cc[i].append(multiply([(x_plus, "b")], h, "cell"))
+        def ev_c(i, h):
+            at["c", i, h] = multiply([(xq[i], "c")] + ([(nq[i], "b")] if i in DIFF else []), h)
 
-        def cell_mix(i):
-            a = work.tile([P, D], F32, name="ca", bufs=CA)
-            ca[i] = a
-            if i in DIFF:
-                for h in range(2):
-                    nc.vector.tensor_tensor(out=a[:, halves[h]], in0=cc[i][2 * h][:], in1=e[i][:, halves[h]], op=ALU.mult)
-                    nc.vector.tensor_tensor(out=a[:, halves[h]], in0=cc[i][2 * h + 1][:], in1=a[:, halves[h]], op=ALU.add)
-                return
-            b = work.tile([P, D], F32, name="cb", bufs=4)
-            for h in range(2):
-                nc.vector.tensor_tensor(out=a[:, halves[h]], in0=cc[i][2 * h][:], in1=e[i][:, halves[h]], op=ALU.mult)
-                nc.vector.scalar_tensor_tensor(
-                    out=b[:, halves[h]], in0=e[i][:, halves[h]], scalar=1.0, in1=cc[i][2 * h + 1][:], op0=ALU.subtract, op1=ALU.mult
-                )
-            cb[i] = b
+        def ev_b(i, h):
+            at["b", i, h] = multiply([(xq[i], "b")], h)
 
-        def cell_sum(i):
-            if i in DIFF:
-                return
-            eng = nc.vector if i in SUM_VECTOR else nc.gpsimd
-            eng.tensor_tensor(out=ca[i][:], in0=ca[i][:], in1=cb[i][:], op=ALU.subtract)
+        def cell(i):
+            if ("ca", i) not in at:
+                at["ca", i] = work.tile([P, D], F32, name="ca", bufs=BUFS["ca"])
+            return at["ca", i]
 
-        def squash(i):
-            nc.scalar.activation(out=ca[i][:], in_=ca[i][:], func=ACT.Tanh)
-
-        def gain_mul(i):
-            hh[i] = work.tile([P, D], BF16, name="hh", bufs=4, align_bytes=64)
-            eng = nc.gpsimd if i in GAIN_POOL else nc.vector
-            if i not in H_PERM:
-                eng.tensor_tensor(out=hh[i][:], in0=ca[i][:], in1=gain[:], op=ALU.mult)
-                return
-            for gg in range(2):
-                eng.tensor_tensor(
-                    out=hh[i][:, halves[gg]].rearrange("p (u m e) -> p u m e", u=2, e=2),
-                    in0=ca[i][:, halves[gg]].rearrange("p (m u e) -> p u m e", u=2, e=2),
-                    in1=gain_perm[:, halves[gg]].rearrange("p (u m e) -> p u m e", u=2, e=2),
-                    op=ALU.mult,
-                )
-
-        def turn_h(i):
-            ht[i] = turn(hh[i], i in H_PERM)
-
-        def collect_h(i):
-            hg[i] = collect(ht[i], "hg", copier(i, HT_SCALAR))
-
-        def quantize_h(i):
-            quantize(hq[i], hq_s[i], hg[i])
-
-        def mark_mm(i):
-            zm[i] = multiply([((hq[i], hq_s[i]), "l")], 0, "cell" if i in M_HELD else "marks")
-
-        def mark_sigmoid(i):
-            nc.scalar.activation(out=e2[:, i, :], in_=zm[i][:], func=ACT.Sigmoid, scale=-1.0)
-
-        stages = dict(
-            widen_x=widen_x, turn_x=turn_x, collect_x=collect_x, quantize_x=quantize_x, negate_x=negate_x, quantize_neg=quantize_neg, rate_mm=rate_mm,
-            rate_sigmoid=rate_sigmoid, rate_ln=rate_ln, rate_mm_again=rate_mm_again, rate_min=rate_min, decay=decay,
-            cell_mm=cell_mm, cell_mix=cell_mix, cell_sum=cell_sum, squash=squash, gain_mul=gain_mul, turn_h=turn_h,
-            collect_h=collect_h, quantize_h=quantize_h, mark_mm=mark_mm, mark_sigmoid=mark_sigmoid,
-        )
-        events = sorted(
-            (first[n // 4] + stride * (n % 4), pos, name, i)
-            for pos, (name, first, stride) in enumerate(PLAN)
-            for n, i in enumerate(P2_ORDER if name in ("rate_ln", "rate_mm_again", "rate_min") else range(TILES))
-        )
-        for step, pos, name, i in events:
-            stages[name](i)
-
-        for i0, count in TAIL:
-            nc.scalar.activation(
-                out=e2[:, i0 : i0 + count, :], in_=e2[:, i0 : i0 + count, :], func=ACT.Ln, bias=tiny[:]
+        def ev_a(i, h):
+            nc.vector.tensor_tensor(
+                out=cell(i)[:, halves[h]], in0=at["c", i, h][:], in1=e[i][:, halves[h]], op=ALU.mult
             )
-            o = work.tile([P, 2, K], F32, name="o", bufs=5)
-            for c in range(count):
-                z2 = zm[i0 + c]
-                if i0 + c not in M_HELD:
-                    z2 = multiply([((hq[i0 + c], hq_s[i0 + c]), "l")], 0, "again" if c else "cell")
-                nc.vector.scalar_tensor_tensor(
-                    out=o[:, c, :], in0=e2[:, i0 + c, :], scalar=-1.0, in1=z2[:], op0=ALU.mult, op1=ALU.max
+
+        def ev_f(i, h):
+            if i in DIFF:
+                a = cell(i)
+                nc.vector.tensor_tensor(out=a[:, halves[h]], in0=at["b", i, h][:], in1=a[:, halves[h]], op=ALU.add)
+                return
+            if ("cb", i) not in at:
+                at["cb", i] = work.tile([P, D], F32, name="cb", bufs=BUFS["cb"])
+            nc.vector.scalar_tensor_tensor(
+                out=at["cb", i][:, halves[h]], in0=e[i][:, halves[h]], scalar=1.0, in1=at["b", i, h][:], op0=ALU.subtract, op1=ALU.mult
+            )
+
+        def ev_u(i):
+            eng = nc.gpsimd if i in GS else nc.vector
+            eng.tensor_tensor(out=cell(i)[:], in0=cell(i)[:], in1=at["cb", i][:], op=ALU.subtract)
+
+        def ev_T(i, h=None):
+            cols = ALL if h is None else halves[h]
+            nc.scalar.activation(out=cell(i)[:, cols], in_=cell(i)[:, cols], func=ACT.Tanh)
+
+        def ev_g(i, gg):
+            if ("hh", i) not in at:
+                at["hh", i] = work.tile([P, D], BF16, name="hh", bufs=BUFS["hh"], align_bytes=64)
+            eng = nc.gpsimd if i in GG else nc.vector
+            eng.tensor_tensor(
+                out=at["hh", i][:, halves[gg]].rearrange("p (u m e) -> p u m e", u=2, e=2),
+                in0=cell(i)[:, halves[gg]].rearrange("p (m u e) -> p u m e", u=2, e=2),
+                in1=gain_sorted[:, halves[gg]].rearrange("p (u m e) -> p u m e", u=2, e=2),
+                op=ALU.mult,
+            )
+
+        def ev_h(i, gg):
+            if ("ht", i) not in at:
+                at["ht", i] = bank()
+            turn(at["ht", i], at["hh", i], gg, True)
+
+        def ev_j(i):
+            at["hg", i] = collect(at["ht", i], "hg", i in HT_S)
+
+        def ev_p(i):
+            quantize(hq[i], at["hg", i])
+
+        def ev_r(i):
+            at["r", i] = multiply([(hq[i], "l")], 0)
+
+        def ev_R(i):
+            nc.scalar.activation(out=e2[i][:], in_=at["r", i][:], func=ACT.Sigmoid, scale=-1.0)
+
+        def ev_v(i):
+            at["v", i] = multiply([(hq[i], "l")], 0)
+
+        def ev_L(i):
+            nc.scalar.activation(out=e2[i][:], in_=e2[i][:], func=ACT.Ln, bias=tiny[:])
+
+        def ev_o(i):
+            z = at["v", i] if ("v", i) in at else at["r", i]
+            o = work.tile([P, K], F32, name="o", bufs=BUFS["o"])
+            nc.vector.scalar_tensor_tensor(
+                out=o[:], in0=e2[i][:], scalar=-1.0, in1=z[:], op0=ALU.mult, op1=ALU.max
+            )
+            nc.sync.dma_start(out=out_rows[:, i, :], in_=o[:])
+
+        def ev_x(i):
+            nc.vector.tensor_copy(out=dt_f[:], in_=dt_bf[:])
+
+        def ev_X(i):
+            for gg in range(2):
+                nc.vector.tensor_copy(
+                    out=gain_sorted[:, halves[gg]].rearrange("p (u m e) -> p u m e", u=2, e=2),
+                    in_=gain[:, halves[gg]].rearrange("p (m u e) -> p u m e", u=2, e=2),
                 )
-            nc.sync.dma_start(out=out_rows[:, i0 : i0 + count, :], in_=o[:, 0:count, :])
+
+        does = dict(
+            w=ev_w, ws=ev_ws, t=ev_t, k=ev_k, q=ev_q, n=ev_n, nq=ev_nq, z=ev_z, s=ev_s, l=ev_l, y=ev_y, m=ev_m, e=ev_e,
+            c=ev_c, b=ev_b, a=ev_a, f=ev_f, u=ev_u, T=ev_T, g=ev_g, h=ev_h, j=ev_j, p=ev_p, r=ev_r, R=ev_R, v=ev_v,
+            L=ev_L, o=ev_o, x=ev_x, X=ev_X,
+        )
+        for item in ORDER.split():
+            part = item.split(".")
+            does[part[0]](*[int(k) for k in part[1:]])

@@ -18,30 +18,17 @@ ALU = mybir.AluOpType
 
 P = 128
 TILES = N // P
-HALF = 512
-TINY = 2.0 ** -62
-XT_S = (0, 1, 2)
-HT_S = (0, 1, 2, 3, 4, 5, 6, 7)
-DIFF = (1, 3, 5, 6, 7)
-GS = (0, 2, 4)
-GG = ()
-BUFS = {'xw': 4, 'xg': 5, 'xn': 2, 'ca': 5, 'cb': 4, 'hh': 4, 'hg': 2, 'o': 8}
-ORDER = """
-w.0 w.1 w.2 ws.0 t.0 t.1 k.0 q.0 t.2 k.1 q.1 w.3 k.2 q.2 w.4 w.5 z.0.0 s.0.0 z.0.1 s.0.1 t.3 k.3 q.3 x.0 w.6
-z.1.0 s.1.0 z.1.1 s.1.1 t.4 k.4 q.4 w.7 z.2.0 s.2.0 z.2.1 s.2.1 t.5 k.5 q.5 z.3.0 s.3.0 z.3.1 s.3.1 t.6 k.6
-q.6 n.1 z.4.0 s.4.0 z.4.1 s.4.1 t.7 k.7 q.7 nq.1 n.3 z.5.0 s.5.0 z.5.1 s.5.1 nq.3 z.6.0 s.6.0 z.6.1 s.6.1 n.5
-z.7.0 s.7.0 z.7.1 s.7.1 l.0 l.1 l.2 nq.5 l.3 n.6 l.4 l.5 nq.6 l.6 n.7 y.0.0 m.0.0 y.0.1 m.0.1 l.7 y.1.0 m.1.0
-y.1.1 m.1.1 e.0 nq.7 y.2.0 m.2.0 y.2.1 m.2.1 e.1 y.3.0 m.3.0 y.3.1 m.3.1 e.2 y.4.0 m.4.0 y.4.1 m.4.1 e.3 y.5.0
-m.5.0 y.5.1 m.5.1 e.4 y.6.0 m.6.0 y.6.1 m.6.1 e.5 y.7.0 m.7.0 y.7.1 m.7.1 X.0 e.6 c.0.0 a.0.0 c.0.1 a.0.1 e.7
-c.1.0 a.1.0 c.1.1 a.1.1 b.0.0 f.0.0 b.0.1 f.0.1 c.2.0 a.2.0 c.2.1 a.2.1 b.1.0 f.1.0 b.1.1 f.1.1 c.3.0 a.3.0
-c.3.1 a.3.1 b.2.0 f.2.0 b.2.1 f.2.1 b.3.0 f.3.0 b.3.1 f.3.1 c.4.0 a.4.0 c.4.1 a.4.1 b.4.0 f.4.0 b.4.1 f.4.1
-u.0 T.0 T.1 g.0.0 g.0.1 g.1.0 g.1.1 c.5.0 a.5.0 c.5.1 a.5.1 b.5.0 f.5.0 b.5.1 f.5.1 u.2 T.2 T.3 g.2.0 g.2.1
-h.0.0 h.0.1 j.0 p.0 c.6.0 a.6.0 c.6.1 a.6.1 g.3.0 g.3.1 h.1.0 h.1.1 b.6.0 f.6.0 b.6.1 f.6.1 u.4 T.4 j.1 p.1
-T.5 h.2.0 h.2.1 j.2 p.2 r.0 R.0 T.6 c.7.0 a.7.0 c.7.1 a.7.1 g.4.0 g.4.1 b.7.0 f.7.0 b.7.1 f.7.1 h.3.0 h.3.1
-j.3 p.3 r.1 R.1 T.7.0 T.7.1 g.5.0 g.5.1 g.6.0 g.6.1 h.4.0 h.4.1 j.4 p.4 r.2 R.2 g.7.0 g.7.1 h.5.0 h.5.1 j.5
-p.5 r.3 R.3 h.6.0 h.6.1 j.6 p.6 r.4 R.4 h.7.0 h.7.1 j.7 p.7 r.5 R.5 r.6 R.6 r.7 R.7 L.0 L.1 v.0 o.0 L.2 v.1
-o.1 L.3 v.2 o.2 L.4 v.3 o.3 L.5 v.4 o.4 L.6 v.5 o.5 o.6 L.7 o.7
-"""
+BANK = 512
+GROUPS = 2
+X_BLOCK = 128
+
+TINY = 2.0**-62
+
+DIFFERENCE_IN_PSUM = (1, 4, 5, 6, 7)
+X_COPY_ON_SCALAR = (0, 1, 2, 3, 4)
+H_COPY_ON_SCALAR = (0, 1, 2, 3, 4, 5, 6)
+MARKS_HELD = (5, 6, 7)
+WARM_UP, WARM_UP_AGAIN = 7, 3
 
 
 def tile_neuralhawkesdecayingcellintensity_d1p_kernel(
@@ -50,285 +37,309 @@ def tile_neuralhawkesdecayingcellintensity_d1p_kernel(
     nc = tc.nc
     with ExitStack() as ctx:
         keep = ctx.enter_context(tc.tile_pool(name="keep", bufs=1))
-        work = ctx.enter_context(tc.tile_pool(name="work", bufs=4))
+        work = ctx.enter_context(tc.tile_pool(name="work", bufs=3))
         psum = ctx.enter_context(tc.psum_pool(name="psum", bufs=8))
         ctx.enter_context(tc.manual_schedule())
 
-        planes = {}
+        halves = (slice(0, BANK), slice(BANK, D))
+
+        def per_tile(name, dtype, width, tiles=range(TILES)):
+            return {i: keep.tile([P, width], dtype, name="%s%d" % (name, i), align_bytes=64) for i in tiles}
+
+        def bank():
+            t = psum.tile([P, BANK], F32, name="bank")
+            return t
+
+        weight_scales = {}
         for w, width in (("d", D), ("c", D), ("b", D), ("l", K)):
-            planes[w] = keep.tile([P, width], U8, name="planes_" + w, align_bytes=64)
-        nc.gpsimd.memset(planes["d"][:].bitcast(I32), 0)
-        ident = keep.tile([P, P], F32, name="ident")
-        make_identity(nc, ident[:])
-        for w in ("c", "b", "l"):
-            nc.gpsimd.memset(planes[w][:].bitcast(I32), 0)
+            weight_scales[w] = keep.tile([P, width], U8, name="scales_" + w, align_bytes=64)
+            nc.gpsimd.memset(weight_scales[w][:].bitcast(I32), 0)
+            if w == "d":
+                ident = keep.tile([P, P], F32, name="ident")
+                make_identity(nc, ident[:])
+        zeros = keep.tile([P, BANK], BF16, name="zeros")
+        nc.vector.memset(zeros[:], 0.0)
         tiny = keep.tile([P, 1], F32, name="tiny")
         nc.vector.memset(tiny[:], TINY)
-        warm = keep.tile([P, 1], F32, name="warm")
-        nc.scalar.activation(out=warm[:], in_=tiny[:], func=ACT.Sigmoid)
+        table = keep.tile([P, 1], F32, name="table")
+        nc.scalar.activation(out=table[:], in_=tiny[:], func=ACT.Sigmoid)
 
         x_rows = x_bytes.rearrange("(p i) k -> p i k", i=TILES)
         out_rows = out.rearrange("(p i) n -> p i n", i=TILES)
-        x_at = {}
+        byte_rows = {}
 
-        def load_x(i0, count):
-            t = keep.tile([P, count, D], U8, name="xb%d" % i0, align_bytes=64)
-            nc.sync.dma_start(out=t[:], in_=x_rows[:, i0 : i0 + count, :])
-            for c in range(count):
-                x_at[i0 + c] = (t, c)
+        def load_x(first, count):
+            t = keep.tile([P, count, D], U8, name="x_bytes%d" % first, align_bytes=64)
+            nc.sync.dma_start(out=t[:], in_=x_rows[:, first : first + count, :])
+            for i in range(count):
+                byte_rows[first + i] = t[:, i, :]
 
         def load_scales(w, scales):
             for q in range(4):
                 nc.sync.dma_start(
-                    out=planes[w][32 * q : 32 * q + 8, :].bitcast(I32),
+                    out=weight_scales[w][32 * q : 32 * q + 8, :].bitcast(I32),
                     in_=scales[:, 4 * q : 4 * q + 4, :].bitcast(I32),
                 )
 
-        w_at = {}
+        weight_words = {}
 
-        def load_words(w, words, c_from, c_to):
-            src = words.rearrange("g p n t -> p g (n t)").bitcast(I32)
-            t = keep.tile([P, 2, c_to - c_from], U32, name="w_%s%d" % (w, c_from), align_bytes=64)
-            nc.sync.dma_start(out=t[:].bitcast(I32), in_=src[:, :, c_from:c_to])
-            for h in range(c_from // HALF, c_to // HALF):
-                w_at[(w, h)] = (t, h - c_from // HALF)
+        def load_words(w, words, first, last):
+            t = keep.tile([P, GROUPS, last - first], U32, name="words_%s%d" % (w, first), align_bytes=64)
+            source = words.rearrange("g p n t -> p g (n t)").bitcast(I32)
+            nc.sync.dma_start(out=t[:].bitcast(I32), in_=source[:, :, first:last])
+            for half in range(first // BANK, last // BANK):
+                columns = slice(BANK * half - first, BANK * half - first + BANK)
+                for gg in range(GROUPS):
+                    weight_words[w, gg, half] = t[:, gg, columns]
 
         load_x(0, 2)
-        xs = keep.tile([P, TILES, 8], F32, name="xs")
-        nc.sync.dma_start(out=xs[:], in_=x_scale.rearrange("(p i) j -> p i j", i=TILES))
+        x_scales = keep.tile([P, TILES, D // X_BLOCK], F32, name="x_scales")
+        nc.sync.dma_start(out=x_scales[:], in_=x_scale.rearrange("(p i) j -> p i j", i=TILES))
         load_scales("d", wd_scales)
-        load_words("d", wd_words, 0, HALF)
+        load_words("d", wd_words, 0, BANK)
         load_x(2, 2)
-        load_words("d", wd_words, HALF, D)
+        load_words("d", wd_words, BANK, D)
         load_x(4, 4)
-        dt_bf = keep.tile([P, TILES], BF16, name="dt_bf")
-        nc.sync.dma_start(out=dt_bf[:], in_=dt.rearrange("(p i) -> p i", i=TILES))
-        gain = keep.tile([P, D], BF16, name="gain")
-        gain_sorted = keep.tile([P, D], BF16, name="gain_sorted")
+        dt_rows = keep.tile([P, TILES], BF16, name="dt_rows")
+        nc.sync.dma_start(out=dt_rows[:], in_=dt.rearrange("(p i) -> p i", i=TILES))
         load_scales("c", wc_scales)
         load_words("c", wc_words, 0, D)
         load_scales("b", wb_scales)
         load_words("b", wb_words, 0, D)
+        gain = keep.tile([P, D], BF16, name="gain")
         nc.sync.dma_start(out=gain[:], in_=g.partition_broadcast(P))
         load_scales("l", wl_scales)
         load_words("l", wl_words, 0, K)
-        dt_f = keep.tile([P, TILES], F32, name="dt_f")
 
-        def row(dtype, width, name):
-            return [keep.tile([P, width], dtype, name="%s%d" % (name, i), align_bytes=64) for i in range(TILES)]
-
-        e = row(F32, D, "e")
-        e2 = row(F32, K, "e2")
-        xq = list(zip(row(U32, 256, "xq"), row(U8, 256, "xqs")))
-        nq = list(zip(row(U32, 256, "nq"), row(U8, 256, "nqs")))
-        hq = list(zip(row(U32, 256, "hq"), row(U8, 256, "hqs")))
-        at = {}
-        halves = (slice(0, HALF), slice(HALF, D))
-        ALL = slice(0, D)
-
-        def bank():
-            t = psum.tile([P, HALF], F32, name="bank")
+        def turn(rows, words_sorted):
+            t = bank()
+            words = rows[:].bitcast(F32)
+            for gg in range(GROUPS):
+                for u in range(2):
+                    if words_sorted:
+                        first = 256 * gg + 128 * u
+                        picked = words[:, first : first + 128]
+                    else:
+                        picked = words[:, 256 * gg + u : 256 * gg + 256 : 2]
+                    nc.tensor.transpose(t[:, 128 * (2 * gg + u) : 128 * (2 * gg + u) + 128], picked, ident[:])
             return t
 
-        def widened(i):
-            if ("xw", i) not in at:
-                at["xw", i] = work.tile([P, D], BF16, name="xw", bufs=BUFS["xw"], align_bytes=64)
-            return at["xw", i]
-
-        def widen(i, blocks, on_scalar):
-            t, c = x_at[i]
-            w = widened(i)
-            for j in blocks:
-                cols = slice(128 * j, 128 * j + 128)
-                src = t[:, c, cols].bitcast(FP8)
-                o = w[:, cols]
-                if i > 0:
-                    gg, m0 = j // 4, 32 * (j % 4)
-                    o = w[:].rearrange("p (g u m e) -> p g m u e", g=2, u=2, e=2)[:, gg, m0 : m0 + 32, :, :]
-                    src = src.rearrange("p (m u e) -> p m u e", u=2, e=2)
-                scale = xs[:, i, j : j + 1]
-                if on_scalar:
-                    nc.scalar.activation(out=o, in_=src, func=ACT.Copy, scale=scale)
-                else:
-                    nc.vector.tensor_scalar(out=o, in0=src, scalar1=scale, scalar2=None, op0=ALU.mult)
-
-        def ev_w(i):
-            widen(i, range(8) if i else range(4), False)
-
-        def ev_ws(i):
-            widen(i, range(4, 8), True)
-
-        def turn(bank_tile, rows, gg, sorted_words):
-            words = rows[:].bitcast(F32)
-            for u in range(2):
-                k = 2 * gg + u
-                if sorted_words:
-                    picked = words[:, 128 * k : 128 * k + 128]
-                else:
-                    picked = words[:, 256 * gg + u : 256 * gg + 256 : 2]
-                nc.tensor.transpose(bank_tile[:, 128 * k : 128 * k + 128], picked, ident[:])
-
-        def ev_t(i):
-            at["xt", i] = bank()
-            for gg in range(2):
-                turn(at["xt", i], at["xw", i], gg, i > 0)
-
-        def collect(t, name, on_scalar):
-            o = work.tile([P, D], BF16, name=name, bufs=BUFS[name], align_bytes=64)
+        def collect(o, t, on_scalar):
             copy = nc.scalar.copy if on_scalar else nc.vector.tensor_copy
             copy(
-                out=o[:].bitcast(F32).rearrange("p (g r u) -> p g r u", g=2, u=2),
-                in_=t[:].rearrange("p (g u r) -> p g r u", g=2, u=2),
+                out=o[:].bitcast(F32).rearrange("p (g r u) -> p g r u", g=GROUPS, u=2),
+                in_=t[:].rearrange("p (g u r) -> p g r u", g=GROUPS, u=2),
             )
-            return o
 
-        def quantize(q, src):
-            nc.vector.quantize_mx(out=q[0][:].bitcast(FP8X4), scales=q[1][:], in_=src[:])
+        def operand(name, tiles=range(TILES)):
+            codes = per_tile(name + "_codes", U32, GROUPS * P, tiles)
+            scales = per_tile(name + "_scales", U8, GROUPS * P, tiles)
+            return {i: (codes[i], scales[i]) for i in tiles}
 
-        def ev_k(i):
-            at["xg", i] = collect(at["xt", i], "xg", i in XT_S)
+        def quantize(target, source):
+            codes, scales = target
+            nc.vector.quantize_mx(out=codes[:].bitcast(FP8X4), scales=scales[:], in_=source[:])
 
-        def ev_q(i):
-            quantize(xq[i], at["xg", i])
-
-        def ev_n(i):
-            at["xn", i] = work.tile([P, D], BF16, name="xn", bufs=BUFS["xn"], align_bytes=64)
-            nc.vector.tensor_scalar(out=at["xn", i][:], in0=at["xg", i][:], scalar1=-1.0, scalar2=None, op0=ALU.mult)
-
-        def ev_nq(i):
-            quantize(nq[i], at["xn", i])
-
-        def multiply(operands, h):
+        def multiply(terms, half):
             t = bank()
-            last = 2 * len(operands) - 1
-            for k in range(last + 1):
-                (codes, scales), w = operands[k // 2]
-                gg = k % 2
-                wt, wh = w_at[(w, h)]
+            passes = [(rows, w, gg) for rows, w in terms for gg in range(GROUPS)]
+            for n, ((codes, scales), w, gg) in enumerate(passes):
+                columns = slice(P * gg, P * gg + P)
                 nc.tensor.matmul_mx(
                     out=t[:],
-                    lhsT=codes[:, 128 * gg : 128 * gg + 128].bitcast(FP8X4),
-                    lhsT_scale=scales[:, 128 * gg : 128 * gg + 128],
-                    rhs=wt[:, gg, HALF * wh : HALF * wh + HALF].bitcast(FP8X4),
-                    rhs_scale=planes[w][4 * gg : P, HALF * h : HALF * h + HALF],
-                    start=(k == 0),
-                    stop=(k == last),
+                    lhsT=codes[:, columns].bitcast(FP8X4),
+                    lhsT_scale=scales[:, columns],
+                    rhs=weight_words[w, gg, half].bitcast(FP8X4),
+                    rhs_scale=weight_scales[w][4 * gg : P, BANK * half : BANK * half + BANK],
+                    start=(n == 0),
+                    stop=(n == len(passes) - 1),
                 )
             return t
 
-        def ev_z(i, h):
-            at["z", i, h] = multiply([(xq[i], "d")], h)
+        def run_steps(jobs):
+            for step in range(TILES + max(behind for job, behind in jobs)):
+                for job, behind in jobs:
+                    if 0 <= step - behind < TILES:
+                        job(step - behind)
 
-        def ev_s(i, h):
-            nc.scalar.activation(out=e[i][:, halves[h]], in_=at["z", i, h][:], func=ACT.Sigmoid, scale=-1.0)
+        x_q = operand("x")
+        x_negative_q = operand("x_negative", DIFFERENCE_IN_PSUM)
+        x_kept = per_tile("x_kept", BF16, D, DIFFERENCE_IN_PSUM)
+        decay = per_tile("decay", F32, D)
+        x_wide = {}
+        x_grouped = {}
 
-        def ev_l(i):
-            nc.scalar.activation(out=e[i][:], in_=e[i][:], func=ACT.Ln, bias=tiny[:])
+        def widen(i):
+            rows = work.tile([P, D], BF16, name="x_wide", bufs=4, align_bytes=64)
+            x_wide[i] = rows
+            by_word = rows[:].rearrange("p (g u m e) -> p g m u e", g=GROUPS, u=2, e=2)
+            for j in range(D // X_BLOCK):
+                columns = slice(X_BLOCK * j, X_BLOCK * j + X_BLOCK)
+                source = byte_rows[i][:, columns].bitcast(FP8)
+                scale = x_scales[:, i, j : j + 1]
+                if i == 0 and j >= 4:
+                    nc.scalar.activation(out=rows[:, columns], in_=source, func=ACT.Copy, scale=scale)
+                    continue
+                target = rows[:, columns]
+                if i > 0:
+                    m = 32 * (j % 4)
+                    target = by_word[:, j // 4, m : m + 32, :, :]
+                    source = source.rearrange("p (m u e) -> p m u e", u=2, e=2)
+                nc.vector.tensor_scalar(out=target, in0=source, scalar1=scale, scalar2=None, op0=ALU.mult)
 
-        def ev_y(i, h):
-            at["y", i, h] = multiply([(xq[i], "d")], h)
+        def turn_x(i):
+            turned = turn(x_wide[i], i > 0)
+            if i in DIFFERENCE_IN_PSUM:
+                x_grouped[i] = x_kept[i]
+            else:
+                t = work.tile([P, D], BF16, name="x_grouped", align_bytes=64)
+                x_grouped[i] = t
+            collect(x_grouped[i], turned, i in X_COPY_ON_SCALAR)
+            if i == 1:
+                warm_up(WARM_UP_AGAIN)
 
-        def ev_m(i, h):
-            z = at["y", i, h] if ("y", i, h) in at else at["z", i, h]
-            nc.vector.scalar_tensor_tensor(
-                out=e[i][:, halves[h]], in0=z[:], scalar=-1.0, in1=e[i][:, halves[h]], op0=ALU.mult, op1=ALU.min
+        def quantize_x(i):
+            quantize(x_q[i], x_grouped[i])
+
+        def rate_sigmoid(i):
+            for half in range(2):
+                z = multiply([(x_q[i], "d")], half)
+                nc.scalar.activation(out=decay[i][:, halves[half]], in_=z[:], func=ACT.Sigmoid, scale=-1.0)
+
+        def warm_up(count):
+            t = bank()
+            for n in range(count):
+                nc.tensor.matmul(t[:], lhsT=zeros[:, 0:P], rhs=zeros[:], start=True, stop=True)
+
+        warm_up(WARM_UP)
+        run_steps(((widen, 0), (turn_x, 2), (rate_sigmoid, 4), (quantize_x, 2)))
+
+        negated = {}
+
+        def negate(i):
+            t = work.tile([P, D], BF16, name="x_negated", align_bytes=64)
+            negated[i] = t
+            nc.vector.tensor_scalar(out=t[:], in0=x_kept[i][:], scalar1=-1.0, scalar2=None, op0=ALU.mult)
+
+        def quantize_negated(i):
+            quantize(x_negative_q[i], negated[i])
+
+        def prepare_negative(tiles):
+            for n, i in enumerate(tiles):
+                negate(i)
+                if n > 0:
+                    quantize_negated(tiles[n - 1])
+            quantize_negated(tiles[-1])
+
+        prepare_negative(DIFFERENCE_IN_PSUM)
+
+        dt_f32 = keep.tile([P, TILES], F32, name="dt_f32")
+        nc.vector.tensor_copy(out=dt_f32[:], in_=dt_rows[:])
+
+        for i in range(TILES):
+            nc.scalar.activation(out=decay[i][:], in_=decay[i][:], func=ACT.Ln, bias=tiny[:])
+        for i in range(TILES):
+            for half in range(2):
+                z = multiply([(x_q[i], "d")], half)
+                nc.vector.scalar_tensor_tensor(
+                    out=decay[i][:, halves[half]],
+                    in0=z[:],
+                    scalar=-1.0,
+                    in1=decay[i][:, halves[half]],
+                    op0=ALU.mult,
+                    op1=ALU.min,
+                )
+            nc.scalar.activation(out=decay[i][:], in_=decay[i][:], func=ACT.Exp, scale=dt_f32[:, i : i + 1])
+
+        gain_sorted = keep.tile([P, D], BF16, name="gain_sorted")
+        for columns in halves:
+            nc.vector.tensor_copy(
+                out=gain_sorted[:, columns].rearrange("p (u m e) -> p u m e", u=2, e=2),
+                in_=gain[:, columns].rearrange("p (m u e) -> p u m e", u=2, e=2),
             )
 
-        def ev_e(i):
-            nc.scalar.activation(out=e[i][:], in_=e[i][:], func=ACT.Exp, scale=dt_f[:, i : i + 1])
+        h_q = operand("h")
+        mark_log = per_tile("mark_log", F32, K)
+        cell = {}
+        h_rows = {}
+        h_grouped = {}
+        marks = {}
 
-        def ev_c(i, h):
-            at["c", i, h] = multiply([(xq[i], "c")] + ([(nq[i], "b")] if i in DIFF else []), h)
+        def mix_first(i):
+            t = work.tile([P, D], F32, name="cell", bufs=8)
+            cell[i] = t
+            terms = [(x_q[i], "c")]
+            if i in DIFFERENCE_IN_PSUM:
+                terms.append((x_negative_q[i], "b"))
+            for half, columns in enumerate(halves):
+                product = multiply(terms, half)
+                nc.vector.tensor_tensor(out=t[:, columns], in0=product[:], in1=decay[i][:, columns], op=ALU.mult)
 
-        def ev_b(i, h):
-            at["b", i, h] = multiply([(xq[i], "b")], h)
-
-        def cell(i):
-            if ("ca", i) not in at:
-                at["ca", i] = work.tile([P, D], F32, name="ca", bufs=BUFS["ca"])
-            return at["ca", i]
-
-        def ev_a(i, h):
-            nc.vector.tensor_tensor(
-                out=cell(i)[:, halves[h]], in0=at["c", i, h][:], in1=e[i][:, halves[h]], op=ALU.mult
-            )
-
-        def ev_f(i, h):
-            if i in DIFF:
-                a = cell(i)
-                nc.vector.tensor_tensor(out=a[:, halves[h]], in0=at["b", i, h][:], in1=a[:, halves[h]], op=ALU.add)
+        def mix_second(i):
+            t = cell[i]
+            if i in DIFFERENCE_IN_PSUM:
+                for half, columns in enumerate(halves):
+                    cbar = multiply([(x_q[i], "b")], half)
+                    nc.vector.tensor_tensor(out=t[:, columns], in0=cbar[:], in1=t[:, columns], op=ALU.add)
                 return
-            if ("cb", i) not in at:
-                at["cb", i] = work.tile([P, D], F32, name="cb", bufs=BUFS["cb"])
-            nc.vector.scalar_tensor_tensor(
-                out=at["cb", i][:, halves[h]], in0=e[i][:, halves[h]], scalar=1.0, in1=at["b", i, h][:], op0=ALU.subtract, op1=ALU.mult
-            )
+            r = work.tile([P, D], F32, name="rest")
+            for half, columns in enumerate(halves):
+                cbar = multiply([(x_q[i], "b")], half)
+                nc.vector.scalar_tensor_tensor(
+                    out=r[:, columns],
+                    in0=decay[i][:, columns],
+                    scalar=1.0,
+                    in1=cbar[:],
+                    op0=ALU.subtract,
+                    op1=ALU.mult,
+                )
+            nc.gpsimd.tensor_tensor(out=t[:], in0=t[:], in1=r[:], op=ALU.subtract)
 
-        def ev_u(i):
-            eng = nc.gpsimd if i in GS else nc.vector
-            eng.tensor_tensor(out=cell(i)[:], in0=cell(i)[:], in1=at["cb", i][:], op=ALU.subtract)
+        def squash(i):
+            for columns in halves if i == TILES - 1 else (slice(0, D),):
+                nc.scalar.activation(out=cell[i][:, columns], in_=cell[i][:, columns], func=ACT.Tanh)
 
-        def ev_T(i, h=None):
-            cols = ALL if h is None else halves[h]
-            nc.scalar.activation(out=cell(i)[:, cols], in_=cell(i)[:, cols], func=ACT.Tanh)
-
-        def ev_g(i, gg):
-            if ("hh", i) not in at:
-                at["hh", i] = work.tile([P, D], BF16, name="hh", bufs=BUFS["hh"], align_bytes=64)
-            eng = nc.gpsimd if i in GG else nc.vector
-            eng.tensor_tensor(
-                out=at["hh", i][:, halves[gg]].rearrange("p (u m e) -> p u m e", u=2, e=2),
-                in0=cell(i)[:, halves[gg]].rearrange("p (m u e) -> p u m e", u=2, e=2),
-                in1=gain_sorted[:, halves[gg]].rearrange("p (u m e) -> p u m e", u=2, e=2),
-                op=ALU.mult,
-            )
-
-        def ev_h(i, gg):
-            if ("ht", i) not in at:
-                at["ht", i] = bank()
-            turn(at["ht", i], at["hh", i], gg, True)
-
-        def ev_j(i):
-            at["hg", i] = collect(at["ht", i], "hg", i in HT_S)
-
-        def ev_p(i):
-            quantize(hq[i], at["hg", i])
-
-        def ev_r(i):
-            at["r", i] = multiply([(hq[i], "l")], 0)
-
-        def ev_R(i):
-            nc.scalar.activation(out=e2[i][:], in_=at["r", i][:], func=ACT.Sigmoid, scale=-1.0)
-
-        def ev_v(i):
-            at["v", i] = multiply([(hq[i], "l")], 0)
-
-        def ev_L(i):
-            nc.scalar.activation(out=e2[i][:], in_=e2[i][:], func=ACT.Ln, bias=tiny[:])
-
-        def ev_o(i):
-            z = at["v", i] if ("v", i) in at else at["r", i]
-            o = work.tile([P, K], F32, name="o", bufs=BUFS["o"])
-            nc.vector.scalar_tensor_tensor(
-                out=o[:], in0=e2[i][:], scalar=-1.0, in1=z[:], op0=ALU.mult, op1=ALU.max
-            )
-            nc.sync.dma_start(out=out_rows[:, i, :], in_=o[:])
-
-        def ev_x(i):
-            nc.vector.tensor_copy(out=dt_f[:], in_=dt_bf[:])
-
-        def ev_X(i):
-            for gg in range(2):
-                nc.vector.tensor_copy(
-                    out=gain_sorted[:, halves[gg]].rearrange("p (u m e) -> p u m e", u=2, e=2),
-                    in_=gain[:, halves[gg]].rearrange("p (m u e) -> p u m e", u=2, e=2),
+        def gain_product(i):
+            t = work.tile([P, D], BF16, name="h_rows", bufs=5, align_bytes=64)
+            h_rows[i] = t
+            for columns in halves:
+                nc.vector.tensor_tensor(
+                    out=t[:, columns].rearrange("p (u m e) -> p u m e", u=2, e=2),
+                    in0=cell[i][:, columns].rearrange("p (m u e) -> p u m e", u=2, e=2),
+                    in1=gain_sorted[:, columns].rearrange("p (u m e) -> p u m e", u=2, e=2),
+                    op=ALU.mult,
                 )
 
-        does = dict(
-            w=ev_w, ws=ev_ws, t=ev_t, k=ev_k, q=ev_q, n=ev_n, nq=ev_nq, z=ev_z, s=ev_s, l=ev_l, y=ev_y, m=ev_m, e=ev_e,
-            c=ev_c, b=ev_b, a=ev_a, f=ev_f, u=ev_u, T=ev_T, g=ev_g, h=ev_h, j=ev_j, p=ev_p, r=ev_r, R=ev_R, v=ev_v,
-            L=ev_L, o=ev_o, x=ev_x, X=ev_X,
+        def turn_h(i):
+            turned = turn(h_rows[i], True)
+            t = work.tile([P, D], BF16, name="h_grouped", bufs=4, align_bytes=64)
+            h_grouped[i] = t
+            collect(t, turned, i in H_COPY_ON_SCALAR)
+
+        def quantize_h(i):
+            quantize(h_q[i], h_grouped[i])
+
+        def marks_sigmoid(i):
+            marks[i] = multiply([(h_q[i], "l")], 0)
+            nc.scalar.activation(out=mark_log[i][:], in_=marks[i][:], func=ACT.Sigmoid, scale=-1.0)
+
+        run_steps(
+            (
+                (mix_second, 1),
+                (marks_sigmoid, 13),
+                (turn_h, 9),
+                (quantize_h, 10),
+                (squash, 2),
+                (gain_product, 6),
+                (mix_first, 0),
+            )
         )
-        for item in ORDER.split():
-            part = item.split(".")
-            does[part[0]](*[int(k) for k in part[1:]])
+
+        for i in range(TILES):
+            nc.scalar.activation(out=mark_log[i][:], in_=mark_log[i][:], func=ACT.Ln, bias=tiny[:])
+            z = marks[i] if i in MARKS_HELD else multiply([(h_q[i], "l")], 0)
+            result = work.tile([P, K], F32, name="result", bufs=8)
+            nc.vector.scalar_tensor_tensor(
+                out=result[:], in0=mark_log[i][:], scalar=-1.0, in1=z[:], op0=ALU.mult, op1=ALU.max
+            )
+            nc.sync.dma_start(out=out_rows[:, i, :], in_=result[:])

from contextlib import ExitStack

import concourse.mybir as mybir
from concourse.masks import make_identity

N, D, K = 1024, 1024, 512
FLOPS = 2 * N * D * (3 * D + K)

F32 = mybir.dt.float32
BF16 = mybir.dt.bfloat16
I32 = mybir.dt.int32
U32 = mybir.dt.uint32
U8 = mybir.dt.uint8
FP8 = mybir.dt.float8_e4m3fn
FP8X4 = mybir.dt.float8_e4m3fn_x4
ACT = mybir.ActivationFunctionType
ALU = mybir.AluOpType

P = 128
TILES = N // P
BANK = 512
GROUPS = 2
X_BLOCK = 128

TINY = 2.0**-62

DIFFERENCE_IN_PSUM = (1, 4, 5, 6, 7)
X_COPY_ON_SCALAR = (0, 1, 2, 3, 4)
H_COPY_ON_SCALAR = (0, 1, 2, 3, 4, 5, 6)
MARKS_HELD = (5, 6, 7)
WARM_UP, WARM_UP_AGAIN = 7, 3


def tile_neuralhawkesdecayingcellintensity_d1p_kernel(
    tc, x_bytes, x_scale, dt, wc_words, wc_scales, wb_words, wb_scales, wd_words, wd_scales, g, wl_words, wl_scales, out
):
    nc = tc.nc
    with ExitStack() as ctx:
        keep = ctx.enter_context(tc.tile_pool(name="keep", bufs=1))
        work = ctx.enter_context(tc.tile_pool(name="work", bufs=3))
        psum = ctx.enter_context(tc.psum_pool(name="psum", bufs=8))
        ctx.enter_context(tc.manual_schedule())

        halves = (slice(0, BANK), slice(BANK, D))

        def per_tile(name, dtype, width, tiles=range(TILES)):
            return {i: keep.tile([P, width], dtype, name="%s%d" % (name, i), align_bytes=64) for i in tiles}

        def bank():
            t = psum.tile([P, BANK], F32, name="bank")
            return t

        weight_scales = {}
        for w, width in (("d", D), ("c", D), ("b", D), ("l", K)):
            weight_scales[w] = keep.tile([P, width], U8, name="scales_" + w, align_bytes=64)
            nc.gpsimd.memset(weight_scales[w][:].bitcast(I32), 0)
            if w == "d":
                ident = keep.tile([P, P], F32, name="ident")
                make_identity(nc, ident[:])
        zeros = keep.tile([P, BANK], BF16, name="zeros")
        nc.vector.memset(zeros[:], 0.0)
        tiny = keep.tile([P, 1], F32, name="tiny")
        nc.vector.memset(tiny[:], TINY)
        table = keep.tile([P, 1], F32, name="table")
        nc.scalar.activation(out=table[:], in_=tiny[:], func=ACT.Sigmoid)

        x_rows = x_bytes.rearrange("(p i) k -> p i k", i=TILES)
        out_rows = out.rearrange("(p i) n -> p i n", i=TILES)
        byte_rows = {}

        def load_x(first, count):
            t = keep.tile([P, count, D], U8, name="x_bytes%d" % first, align_bytes=64)
            nc.sync.dma_start(out=t[:], in_=x_rows[:, first : first + count, :])
            for i in range(count):
                byte_rows[first + i] = t[:, i, :]

        def load_scales(w, scales):
            for q in range(4):
                nc.sync.dma_start(
                    out=weight_scales[w][32 * q : 32 * q + 8, :].bitcast(I32),
                    in_=scales[:, 4 * q : 4 * q + 4, :].bitcast(I32),
                )

        weight_words = {}

        def load_words(w, words, first, last):
            t = keep.tile([P, GROUPS, last - first], U32, name="words_%s%d" % (w, first), align_bytes=64)
            source = words.rearrange("g p n t -> p g (n t)").bitcast(I32)
            nc.sync.dma_start(out=t[:].bitcast(I32), in_=source[:, :, first:last])
            for half in range(first // BANK, last // BANK):
                columns = slice(BANK * half - first, BANK * half - first + BANK)
                for gg in range(GROUPS):
                    weight_words[w, gg, half] = t[:, gg, columns]

        load_x(0, 2)
        x_scales = keep.tile([P, TILES, D // X_BLOCK], F32, name="x_scales")
        nc.sync.dma_start(out=x_scales[:], in_=x_scale.rearrange("(p i) j -> p i j", i=TILES))
        load_scales("d", wd_scales)
        load_words("d", wd_words, 0, BANK)
        load_x(2, 2)
        load_words("d", wd_words, BANK, D)
        load_x(4, 4)
        dt_rows = keep.tile([P, TILES], BF16, name="dt_rows")
        nc.sync.dma_start(out=dt_rows[:], in_=dt.rearrange("(p i) -> p i", i=TILES))
        load_scales("c", wc_scales)
        load_words("c", wc_words, 0, D)
        load_scales("b", wb_scales)
        load_words("b", wb_words, 0, D)
        gain = keep.tile([P, D], BF16, name="gain")
        nc.sync.dma_start(out=gain[:], in_=g.partition_broadcast(P))
        load_scales("l", wl_scales)
        load_words("l", wl_words, 0, K)

        def turn(rows, words_sorted):
            t = bank()
            words = rows[:].bitcast(F32)
            for gg in range(GROUPS):
                for u in range(2):
                    if words_sorted:
                        first = 256 * gg + 128 * u
                        picked = words[:, first : first + 128]
                    else:
                        picked = words[:, 256 * gg + u : 256 * gg + 256 : 2]
                    nc.tensor.transpose(t[:, 128 * (2 * gg + u) : 128 * (2 * gg + u) + 128], picked, ident[:])
            return t

        def collect(o, t, on_scalar):
            copy = nc.scalar.copy if on_scalar else nc.vector.tensor_copy
            copy(
                out=o[:].bitcast(F32).rearrange("p (g r u) -> p g r u", g=GROUPS, u=2),
                in_=t[:].rearrange("p (g u r) -> p g r u", g=GROUPS, u=2),
            )

        def operand(name, tiles=range(TILES)):
            codes = per_tile(name + "_codes", U32, GROUPS * P, tiles)
            scales = per_tile(name + "_scales", U8, GROUPS * P, tiles)
            return {i: (codes[i], scales[i]) for i in tiles}

        def quantize(target, source):
            codes, scales = target
            nc.vector.quantize_mx(out=codes[:].bitcast(FP8X4), scales=scales[:], in_=source[:])

        def multiply(terms, half):
            t = bank()
            passes = [(rows, w, gg) for rows, w in terms for gg in range(GROUPS)]
            for n, ((codes, scales), w, gg) in enumerate(passes):
                columns = slice(P * gg, P * gg + P)
                nc.tensor.matmul_mx(
                    out=t[:],
                    lhsT=codes[:, columns].bitcast(FP8X4),
                    lhsT_scale=scales[:, columns],
                    rhs=weight_words[w, gg, half].bitcast(FP8X4),
                    rhs_scale=weight_scales[w][4 * gg : P, BANK * half : BANK * half + BANK],
                    start=(n == 0),
                    stop=(n == len(passes) - 1),
                )
            return t

        def run_steps(jobs):
            for step in range(TILES + max(behind for job, behind in jobs)):
                for job, behind in jobs:
                    if 0 <= step - behind < TILES:
                        job(step - behind)

        x_q = operand("x")
        x_negative_q = operand("x_negative", DIFFERENCE_IN_PSUM)
        x_kept = per_tile("x_kept", BF16, D, DIFFERENCE_IN_PSUM)
        decay = per_tile("decay", F32, D)
        x_wide = {}
        x_grouped = {}

        def widen(i):
            rows = work.tile([P, D], BF16, name="x_wide", bufs=4, align_bytes=64)
            x_wide[i] = rows
            by_word = rows[:].rearrange("p (g u m e) -> p g m u e", g=GROUPS, u=2, e=2)
            for j in range(D // X_BLOCK):
                columns = slice(X_BLOCK * j, X_BLOCK * j + X_BLOCK)
                source = byte_rows[i][:, columns].bitcast(FP8)
                scale = x_scales[:, i, j : j + 1]
                if i == 0 and j >= 4:
                    nc.scalar.activation(out=rows[:, columns], in_=source, func=ACT.Copy, scale=scale)
                    continue
                target = rows[:, columns]
                if i > 0:
                    m = 32 * (j % 4)
                    target = by_word[:, j // 4, m : m + 32, :, :]
                    source = source.rearrange("p (m u e) -> p m u e", u=2, e=2)
                nc.vector.tensor_scalar(out=target, in0=source, scalar1=scale, scalar2=None, op0=ALU.mult)

        def turn_x(i):
            turned = turn(x_wide[i], i > 0)
            if i in DIFFERENCE_IN_PSUM:
                x_grouped[i] = x_kept[i]
            else:
                t = work.tile([P, D], BF16, name="x_grouped", align_bytes=64)
                x_grouped[i] = t
            collect(x_grouped[i], turned, i in X_COPY_ON_SCALAR)
            if i == 1:
                warm_up(WARM_UP_AGAIN)

        def quantize_x(i):
            quantize(x_q[i], x_grouped[i])

        def rate_sigmoid(i):
            for half in range(2):
                z = multiply([(x_q[i], "d")], half)
                nc.scalar.activation(out=decay[i][:, halves[half]], in_=z[:], func=ACT.Sigmoid, scale=-1.0)

        def warm_up(count):
            t = bank()
            for n in range(count):
                nc.tensor.matmul(t[:], lhsT=zeros[:, 0:P], rhs=zeros[:], start=True, stop=True)

        warm_up(WARM_UP)
        run_steps(((widen, 0), (turn_x, 2), (rate_sigmoid, 4), (quantize_x, 2)))

        negated = {}

        def negate(i):
            t = work.tile([P, D], BF16, name="x_negated", align_bytes=64)
            negated[i] = t
            nc.vector.tensor_scalar(out=t[:], in0=x_kept[i][:], scalar1=-1.0, scalar2=None, op0=ALU.mult)

        def quantize_negated(i):
            quantize(x_negative_q[i], negated[i])

        def prepare_negative(tiles):
            for n, i in enumerate(tiles):
                negate(i)
                if n > 0:
                    quantize_negated(tiles[n - 1])
            quantize_negated(tiles[-1])

        prepare_negative(DIFFERENCE_IN_PSUM)

        dt_f32 = keep.tile([P, TILES], F32, name="dt_f32")
        nc.vector.tensor_copy(out=dt_f32[:], in_=dt_rows[:])

        for i in range(TILES):
            nc.scalar.activation(out=decay[i][:], in_=decay[i][:], func=ACT.Ln, bias=tiny[:])
        for i in range(TILES):
            for half in range(2):
                z = multiply([(x_q[i], "d")], half)
                nc.vector.scalar_tensor_tensor(
                    out=decay[i][:, halves[half]],
                    in0=z[:],
                    scalar=-1.0,
                    in1=decay[i][:, halves[half]],
                    op0=ALU.mult,
                    op1=ALU.min,
                )
            nc.scalar.activation(out=decay[i][:], in_=decay[i][:], func=ACT.Exp, scale=dt_f32[:, i : i + 1])

        gain_sorted = keep.tile([P, D], BF16, name="gain_sorted")
        for columns in halves:
            nc.vector.tensor_copy(
                out=gain_sorted[:, columns].rearrange("p (u m e) -> p u m e", u=2, e=2),
                in_=gain[:, columns].rearrange("p (m u e) -> p u m e", u=2, e=2),
            )

        h_q = operand("h")
        mark_log = per_tile("mark_log", F32, K)
        cell = {}
        h_rows = {}
        h_grouped = {}
        marks = {}

        def mix_first(i):
            t = work.tile([P, D], F32, name="cell", bufs=8)
            cell[i] = t
            terms = [(x_q[i], "c")]
            if i in DIFFERENCE_IN_PSUM:
                terms.append((x_negative_q[i], "b"))
            for half, columns in enumerate(halves):
                product = multiply(terms, half)
                nc.vector.tensor_tensor(out=t[:, columns], in0=product[:], in1=decay[i][:, columns], op=ALU.mult)

        def mix_second(i):
            t = cell[i]
            if i in DIFFERENCE_IN_PSUM:
                for half, columns in enumerate(halves):
                    cbar = multiply([(x_q[i], "b")], half)
                    nc.vector.tensor_tensor(out=t[:, columns], in0=cbar[:], in1=t[:, columns], op=ALU.add)
                return
            r = work.tile([P, D], F32, name="rest")
            for half, columns in enumerate(halves):
                cbar = multiply([(x_q[i], "b")], half)
                nc.vector.scalar_tensor_tensor(
                    out=r[:, columns],
                    in0=decay[i][:, columns],
                    scalar=1.0,
                    in1=cbar[:],
                    op0=ALU.subtract,
                    op1=ALU.mult,
                )
            nc.gpsimd.tensor_tensor(out=t[:], in0=t[:], in1=r[:], op=ALU.subtract)

        def squash(i):
            for columns in halves if i == TILES - 1 else (slice(0, D),):
                nc.scalar.activation(out=cell[i][:, columns], in_=cell[i][:, columns], func=ACT.Tanh)

        def gain_product(i):
            t = work.tile([P, D], BF16, name="h_rows", bufs=5, align_bytes=64)
            h_rows[i] = t
            for columns in halves:
                nc.vector.tensor_tensor(
                    out=t[:, columns].rearrange("p (u m e) -> p u m e", u=2, e=2),
                    in0=cell[i][:, columns].rearrange("p (m u e) -> p u m e", u=2, e=2),
                    in1=gain_sorted[:, columns].rearrange("p (u m e) -> p u m e", u=2, e=2),
                    op=ALU.mult,
                )

        def turn_h(i):
            turned = turn(h_rows[i], True)
            t = work.tile([P, D], BF16, name="h_grouped", bufs=4, align_bytes=64)
            h_grouped[i] = t
            collect(t, turned, i in H_COPY_ON_SCALAR)

        def quantize_h(i):
            quantize(h_q[i], h_grouped[i])

        def marks_sigmoid(i):
            marks[i] = multiply([(h_q[i], "l")], 0)
            nc.scalar.activation(out=mark_log[i][:], in_=marks[i][:], func=ACT.Sigmoid, scale=-1.0)

        run_steps(
            (
                (mix_second, 1),
                (marks_sigmoid, 13),
                (turn_h, 9),
                (quantize_h, 10),
                (squash, 2),
                (gain_product, 6),
                (mix_first, 0),
            )
        )

        for i in range(TILES):
            nc.scalar.activation(out=mark_log[i][:], in_=mark_log[i][:], func=ACT.Ln, bias=tiny[:])
            z = marks[i] if i in MARKS_HELD else multiply([(h_q[i], "l")], 0)
            result = work.tile([P, K], F32, name="result", bufs=8)
            nc.vector.scalar_tensor_tensor(
                out=result[:], in0=mark_log[i][:], scalar=-1.0, in1=z[:], op0=ALU.mult, op1=ALU.max
            )
            nc.sync.dma_start(out=out_rows[:, i, :], in_=result[:])
